import numpy as np, ml_dtypes
CORES = [48,51,52,55]
N = 4
BF = ml_dtypes.bfloat16
def gentries(a):
    return np.ascontiguousarray(a.reshape(8, 16, -1).transpose(0, 2, 1)).reshape(8, -1)
def gtable(e):
    e = np.asarray(e); return np.ascontiguousarray(e.reshape(8, -1, 16).transpose(0, 2, 1)).reshape(128, -1).astype(np.int32)
V, E, R, B = 1024, 512, 4, 4
W = N * V
def parts(rng):
    m = np.floor(rng.random((8, 16, W)) * rng.choice(np.array([2, 3, 6, 16]), (8, 1, W))).astype(np.int64)
    ring = rng.integers(0, W, (N, 8, R, V)); u = np.ascontiguousarray(np.argsort(rng.random((N, 8, B, V)), axis=-1)[..., :E])
    return m, ring, u, rng.integers(0, W, (N, 8, B, E))
def pack(m, ring, u, v):
    return {"m0": np.repeat(m.reshape(1, 128, W), N, axis=0).astype(BF), "ring0": np.ascontiguousarray(ring.reshape(N, 8 * R, V)).astype(np.int32),
            "eu": np.stack([gtable(a.reshape(8, -1)) for a in u]), "ev": np.stack([gtable(a.reshape(8, -1)) for a in v])}
def setup_inputs(rng):
    return pack(*parts(rng))
def setup_inputs_ties(rng):
    m, ring, u, v = parts(rng)
    for g in range(8):
        if g % 4 == 0:
            for k in range(R): ring[:, g, k] = ring[:, g, k // 2 * 2]
        if g % 4 == 1: ring[:, g] = ring[:, g, :1]
        if g % 4 == 2: m[g] = rng.integers(0, 16, (16, 3))[:, rng.integers(0, 3, W)]
        if g % 4 == 3: m[g] = rng.integers(0, 2, (16, W)) * rng.integers(0, 2, (1, W))
    return pack(m, ring, u, v)
def setup_inputs_after(rng):
    m, ring, u, v = parts(rng)
    u[:, 4:6] = np.take_along_axis(np.repeat(u[:, 4:6, :1], B, axis=2), np.argsort(rng.random((N, 2, B, E)), axis=-1), axis=-1)
    nodes = u + np.arange(N).reshape(N, 1, 1, 1) * V
    for q in range(N):
        o = (q + int(rng.integers(1, N))) % N
        v[q, ::2, 1:] = nodes[o, ::2, :-1]; v[q, 1::2] = nodes[o, 1::2]
    return pack(m, ring, u, v)
def setup_inputs_alike(rng):
    m, ring, u, v = parts(rng); own = np.arange(N).reshape(N, 1, 1) * V
    v[:, :2] = rng.integers(0, W, (N, 2, B, 1))
    for q in range(N): ring[q, 1] = rng.integers(0, V, (R, V)) + (q + int(rng.integers(1, N))) % N * V
    v[:, 2] = u[:, 2] + own
    ring[:, 3] = np.arange(V) + own
    hot = int(rng.integers(0, W)); ring[:, 4] = hot; m[4, :, hot] = rng.integers(1, 16, 16)
    ring[:, 5] = rng.integers(0, V, (N, R, V)) + own; v[:, 5] = rng.integers(0, V, (N, B, E)) + own
    ring[:, 6] = (rng.integers(V, W, (N, R, V)) + own) % W; v[:, 6] = (rng.integers(V, W, (N, B, E)) + own) % W
    u[:, 7] = np.arange(E); u[:, 7, 1] = np.arange(V - E, V)
    first = int(rng.integers(0, N)) * V; ring[:, 7] = rng.integers(0, V, (N, R, V)) + first; v[:, 7] = rng.integers(0, V, (N, B, E)) + first
    return pack(m, ring, u, v)
def setup_inputs_ends(rng):
    m, ring, u, v = parts(rng)
    m = 15 * (rng.random((8, 16, W)) < rng.choice(np.array([0.1, 0.5, 1.0]), (8, 1, W))).astype(np.int64); m[0] = 15; m[1] = 0
    m[2:4] = rng.integers(12, 15, (2, 16, 1)) + rng.integers(-1, 2, (2, 16, W)) * (rng.random((2, 16, W)) < np.array([1.0, 0.125]).reshape(2, 1, 1))
    mid = np.argsort(rng.random((N, 8, B, V - 2)), axis=-1)[..., :E - 2] + 1
    u = np.concatenate([np.full((N, 8, B, 1), V - 1), mid, np.zeros((N, 8, B, 1), np.int64)], axis=3)
    ends = np.concatenate([np.arange(N) * V, np.arange(N) * V + V - 1])
    ring[:, 5:] = rng.choice(ends, (N, 3, R, V)); v[:, 5:] = rng.choice(ends, (N, 3, B, E))
    return pack(m, ring, u, v)
def setup_inputs_spread(rng):
    m, ring, u, v = parts(rng)
    m = np.floor(16 * rng.random((8, 16, W)) * np.exp2(-rng.integers(0, 5, (8, 1, W)))).astype(np.int64)
    o = np.argsort(rng.random((8, W)), axis=-1)
    for g in range(8):
        ring[:, g] = o[g][np.minimum((W * rng.random((N, R, V)) ** 4).astype(np.int64), W - 1)]
        v[:, g] = o[g][np.minimum((W * rng.random((N, B, E)) ** 4).astype(np.int64), W - 1)]
    u = np.ascontiguousarray(np.argsort(rng.random((N, 8, B, V)) * np.exp2(3 * rng.random((N, 8, 1, V))), axis=-1)[..., :E])
    return pack(m, ring, u, v)
def check_inputs(d):
    bad = []; a = np.asarray(d["m0"]).astype(np.float32)
    if not np.all((a >= 0) & (a <= 15) & (a == np.floor(a))): bad.append("range of m0")
    if not np.all(a == a[:1]): bad.append("m0 alike on all ranks")
    for k, hi in (("ring0", W - 1), ("eu", V - 1), ("ev", W - 1)):
        if np.min(d[k]) < 0 or np.max(d[k]) > hi: bad.append("range of " + k)
    s = np.sort(np.stack([gentries(x) for x in d["eu"]]).reshape(N, 8, B, E), axis=-1)
    if np.any(s[..., 1:] == s[..., :-1]): bad.append("u distinct in a batch")
    return bad
def reference(m0, ring0, eu, ev):
    m = m0[0].astype(np.int64).reshape(8, 16, W); ring = ring0.astype(np.int64).reshape(N, 8, R, V).copy(); gi = np.arange(8)[:, None]
    us = np.stack([gentries(a) for a in eu]).astype(np.int64).reshape(N, 8, B, E); vs = np.stack([gentries(a) for a in ev]).astype(np.int64).reshape(N, 8, B, E)
    for b in range(B):
        new = m.copy()
        for q in range(N):
            u, v = us[q, :, b], vs[q, :, b]
            ids = np.take_along_axis(ring[q], np.broadcast_to(u[:, None, :], (8, R, E)), 2)
            mi = np.take_along_axis(m, ids.reshape(8, 1, R * E), 2).reshape(8, 16, R, E)
            mu = np.take_along_axis(m, u[:, None, :] + q * V, 2); mv = np.take_along_axis(m, v[:, None, :], 2)
            c = np.sum(mi * mv[:, :, None, :], axis=1)
            k = np.argmin(c, axis=1)
            np.put_along_axis(new, np.broadcast_to(u[:, None, :] + q * V, (8, 16, E)), np.clip(mu + mv - np.max(mi, axis=2), 0, 15), 2)
            ring[q][gi, k, u] = v
        m = new
    full = m.reshape(128, W)
    return {"ym": np.stack([full[:, q * V:(q + 1) * V] for q in range(N)]).astype(BF), "yr": ring.reshape(N, 8 * R, V).astype(np.float32)}

@@ -1,0 +1,343 @@
+from concourse.bass import DstId, RemoteDMATransfer
+from concourse.mybir import AluOpType as A, ActivationFunctionType as F
+
+NB, V, E, R = 4, 1024, 512, 4
+NCH = 4
+PM = (9, 9, 12, 16)
+BF, F32, I32, U16 = "bfloat16", "float32", "int32", "uint16"
+
+SCRATCH = {
+    "OB": ("sbuf", [128, V + NB * E], BF),
+    "RW": ("sbuf", [128, V + NB * E], F32),
+    "RI": ("sbuf", [128, V], I32),
+    "LL": ("sbuf", [128, V + E], F32),
+    "IE": ("sbuf", [128, E], F32),
+    "EUI": ("sbuf", [128, 128], I32), "EVI": ("sbuf", [128, 128], I32),
+    "EU16": ("sbuf", [128, 128], U16), "EV16": ("sbuf", [128, 128], U16), "EVF": ("sbuf", [128, 128], F32),
+    "MX": ("sbuf", [128, 2048], BF), "PR": ("sbuf", [128, 2048], BF),
+    "SS": ("sbuf", [128, 512], BF), "SG": ("sbuf", [128, 512], BF), "ON": ("sbuf", [128, 128], F32),
+    "XM": ("sbuf", [128, 512], F32), "XS": ("sbuf", [128, 512], F32), "DF": ("sbuf", [128, 128], F32),
+    "VW": ("sbuf", [128, 512], F32),
+    "YB": ("sbuf", [128, V], BF), "YR": ("sbuf", [128, V], F32),
+    "ONE": ("sbuf", [128, 128], BF), "ID": ("sbuf", [128, 128], BF), "IF": ("sbuf", [128, 128], F32),
+    "DI": ("sbuf", [128, 16, 128], F32), "RQ": ("sbuf", [128, 16], F32), "CI": ("sbuf", [128, 16], F32),
+    "LE": ("sbuf", [128, 4, 128], F32), "LV": ("sbuf", [128, 4, 128], F32),
+    "BO": ("sbuf", [128, 8, 4, 4], BF), "B1": ("sbuf", [128, 128], BF),
+    "LD": ("sbuf", [128, 4, 8, 4, 4], BF), "SK": ("sbuf", [128, 8, 4, 4], F32), "S2": ("sbuf", [128, 2, 128], F32),
+    "LS": ("sbuf", [128, 4, 8, 4, 4], BF),
+    "Q4": ("sbuf", [128, 512], F32), "MK": ("sbuf", [128, 512], F32), "RS": ("sbuf", [128, 512], BF),
+    "PC": ("sbuf", [128, 4], I32), "CF": ("sbuf", [128, 4], F32),
+    "W": ("psum", [128, 512], F32), "DB": ("psum", [128, 512], F32), "CX": ("psum", [128, 512], F32), "LX": ("psum", [128, 512], F32),
+}
+for _c in range(4):
+    SCRATCH["TB%d" % _c] = ("sbuf", [128, 4 * V], BF)
+    SCRATCH["OF%d" % _c] = ("sbuf", [128, 128], U16)
+    SCRATCH["LW%d" % _c] = ("sbuf", [128, 96], U16)
+    SCRATCH["MR%d" % _c] = ("psum", [128, 512], F32)
+for _c in range(2):
+    SCRATCH["MU%d" % _c] = ("sbuf", [128, 512], BF)
+    SCRATCH["MV%d" % _c] = ("sbuf", [128, 512], BF)
+    SCRATCH["MT%d" % _c] = ("sbuf", [128, 2048], BF)
+NDMA = 24
+SEMAPHORES = ["cv", "cs", "cp", "cg", "sent"] + ["arr%d" % b for b in range(NB)] + ["d%d" % i for i in range(NDMA)]
+
+
+def rank_program(g, core, T, topo):
+    rank = T.rank_of(core)
+    if rank is None:
+        return
+    peers = [c for c in T.cores if c != core]
+    own = rank * V
+    QU = {"v": g.vector, "s": g.scalar, "p": g.tensor, "g": g, "y": g.sync}
+    known = {q: {} for q in QU}
+    total, waited, acc, ndma = {}, {}, {}, [0]
+    psum = {n for n in SCRATCH if SCRATCH[n][0] == "psum"}
+
+    def wait(q, rec):
+        sem, val, clk = rec
+        if known[q].get(sem, 0) >= val:
+            return
+        QU[q].wait_ge(T.sem[sem], val)
+        waited[sem] = max(waited.get(sem, 0), val)
+        for s, x in clk.items():
+            known[q][s] = max(known[q].get(s, 0), x)
+        known[q][sem] = max(known[q].get(sem, 0), val)
+
+    def order(q, reads, writes, dma=False, waw=False):
+        deps = []
+        for mode, regs in ((0, reads), (1, writes)):
+            for (b, c0, c1) in regs:
+                for (aq, aw, a0, a1, rec) in acc.get(b, []):
+                    ps = b in psum
+                    hit = a1 > c0 and c1 > a0
+                    if not ps and not hit:
+                        continue
+                    same = aq == q and not dma
+                    if mode == 0 and ((aw and hit) or (ps and not same)):
+                        deps.append(rec)
+                    elif mode == 1 and (not same or (aw and waw)):
+                        deps.append(rec)
+        for rec in sorted(deps, key=lambda x: -sum(x[2].values()) - x[1]):
+            wait(q, rec)
+
+    def note(q, rec, reads, writes):
+        for w, regs in ((False, reads), (True, writes)):
+            for (b, c0, c1) in regs:
+                lst = acc.setdefault(b, [])
+                if w and b not in psum:
+                    lst[:] = [x for x in lst if not (c0 <= x[2] and x[3] <= c1)]
+                lst.append((q, w, c0, c1, rec))
+
+    def op(q, fn, reads, writes, waw=False):
+        order(q, reads, writes, waw=waw)
+        sem = "c" + q
+        fn(QU[q]).then_inc(T.sem[sem], 1)
+        total[sem] = total.get(sem, 0) + 1
+        rec = (sem, total[sem], dict(known[q]))
+        note(q, rec, reads, writes)
+        return rec
+
+    def dmas(parts, reads, writes):
+        sem = "d%d" % ndma[0]
+        ndma[0] += 1
+        clk = {}
+        for q, out, in_ in parts:
+            order(q, reads, writes, dma=True)
+            QU[q].dma_start(out, in_).then_inc(T.sem[sem], 16)
+            for s, x in known[q].items():
+                clk[s] = max(clk.get(s, 0), x)
+        total[sem] = 16 * len(parts)
+        note("dma" + sem, (sem, total[sem], clk), reads, writes)
+
+    def full(n):
+        c = 1
+        for d in SCRATCH[n][1][1:]:
+            c *= d
+        return (n, 0, c)
+
+    def mm(out, lhsT, rhs, start, stop, reads, writes):
+        op("p", lambda e: e.matmul(out, lhsT, rhs, start, stop), reads, writes)
+
+    def gath(q, out, win, off, reads, writes):
+        if q == "v":
+            return op(q, lambda e: e.tensor_copy(out, win.indirect(off)), reads, writes)
+        return op(q, lambda e: e.activation(out, win.indirect(off), F.Copy), reads, writes)
+
+    dmas([("y", T.EUI[:], T.eu[:])], [], [full("EUI")])
+    dmas([("s", T.EVI[:], T.ev[:])], [], [full("EVI")])
+    dmas([("sy"[i % 2], T.RI[i::16, :], T.ring0[i % 4::4, :]) for i in range(16)], [], [full("RI")])
+    dmas([("sy"[i % 2], T.TB0[:, i * V:(i + 1) * V], T.m0[:, i * V:(i + 1) * V]) for i in range(4)], [], [full("TB0")])
+    dmas([("y", T.OB[:, 0:V], T.m0[:, own:own + V])], [], [("OB", 0, V)])
+
+    def sel(out, in_, pat, cmp, base, cm):
+        return lambda e: e.affine_select(out, in_, pat, cmp, 0.0, base, cm)
+
+    one = T.ONE[:]
+    op("v", lambda e: e.memset(one, 1.0), [], [full("ONE")])
+    op("g", lambda e: e.iota(T.PC[:, 0:1], [[0, 1]], 0, 1), [], [("PC", 0, 1)])
+    op("g", lambda e: e.iota(T.RQ[:], [[1, 16]], 0, 0, allow_small_or_imprecise_dtypes=True), [], [full("RQ")])
+    op("g", sel(T.B1[:], one, [[-16, 8], [0, 16]], A.is_ge, 0, 1), [full("ONE")], [full("B1")])
+    op("g", sel(T.BO[:], T.B1[:], [[16, 8], [0, 16]], A.is_ge, 15, -1), [full("B1")], [full("BO")])
+    op("g", sel(T.IF[:], one, [[-1, 128]], A.is_equal, 0, 1), [full("ONE")], [full("IF")])
+    for a in range(4):
+        op("g", sel(T.LE[:, a, :], one, [[-16, 8], [0, 4], [-1, 4]], A.is_equal, -4 * a, 1), [full("ONE")], [("LE", 128 * a, 128 * a + 128)])
+    op("g", lambda e: e.iota(T.IE[:], [[1, E]], 0, 0, allow_small_or_imprecise_dtypes=True), [], [full("IE")])
+    op("g", lambda e: e.iota(T.LL[:, 0:V], [[1, V]], 0, 0, allow_small_or_imprecise_dtypes=True), [], [("LL", 0, V)])
+    op("g", sel(T.ID[:], one, [[-1, 128]], A.is_equal, 0, 1), [full("ONE")], [full("ID")])
+    for z in range(4):
+        op("g", sel(T.LV[:, z, :], one, [[-16, 8], [-1, 4], [0, 4]], A.is_equal, -4 * z, 1), [full("ONE")], [("LV", 128 * z, 128 * z + 128)])
+
+    op("v", lambda e: e.tensor_scalar(T.PC[:, 1:2], T.PC[:, 0:1], 3, None, A.bitwise_and), [("PC", 0, 1)], [("PC", 1, 2)])
+    op("v", lambda e: e.tensor_scalar(T.PC[:, 2:3], T.PC[:, 0:1], 2, 3, A.logical_shift_right, A.bitwise_and), [("PC", 0, 1)], [("PC", 2, 3)])
+    op("v", lambda e: e.tensor_scalar(T.PC[:, 3:4], T.PC[:, 0:1], 15, None, A.bitwise_and), [("PC", 0, 1)], [("PC", 3, 4)])
+    for a in range(4):
+        op("v", lambda e: e.memset(T.Q4[:, a::4], float(a)), [], [full("Q4")])
+    op("v", lambda e: e.tensor_copy(T.CF[:, 3:4], T.PC[:, 3:4]), [("PC", 3, 4)], [("CF", 3, 4)])
+    op("v", lambda e: e.tensor_copy(T.CF[:, 0:1], T.PC[:, 2:3]), [("PC", 2, 3)], [("CF", 0, 1)])
+    op("v", lambda e: e.tensor_tensor(T.CF[:, 1:2], T.PC[:, 2:3], T.PC[:, 1:2], A.is_ge), [("PC", 1, 3)], [("CF", 1, 2)])
+    op("v", lambda e: e.memset(T.RS[:], 1.0), [], [full("RS")])
+    op("v", lambda e: e.tensor_scalar(T.CI[:], T.RQ[:], T.CF[:, 3:4], None, A.is_equal), [full("RQ"), ("CF", 3, 4)], [full("CI")])
+    op("v", lambda e: e.tensor_scalar(T.CF[:, 2:3], T.CF[:, 1:2], -0.5, None, A.add), [("CF", 1, 2)], [("CF", 2, 3)])
+    op("v", lambda e: e.tensor_scalar(T.MK[:], T.Q4[:], T.CF[:, 0:1], None, A.is_equal), [full("Q4"), ("CF", 0, 1)], [full("MK")])
+    op("v", lambda e: e.memset(T.RS[:, 0::4], 0.0), [], [full("RS")], waw=True)
+    op("v", lambda e: e.memset(T.LD[:], 0.0), [], [full("LD")])
+    for i in range(16):
+        op("s", lambda e: e.activation(T.DI[:, i, :], T.IF[:], F.Copy, scale=T.CI[:, i:i + 1]), [full("IF"), full("CI")], [("DI", 128 * i, 128 * i + 128)])
+    for k in range(4):
+        op("v", lambda e: e.tensor_scalar(T.LD[:, k, :, :, k], T.BO[:, :, :, k], -1.0, None, A.mult), [full("BO")], [full("LD")], waw=(k == 0))
+    op("v", lambda e: e.tensor_copy(T.EU16[:], T.EUI[:]), [full("EUI")], [full("EU16")])
+    for k in range(4):
+        op("v", lambda e: e.tensor_copy(T.LD[:, k, :, k, :], T.BO[:, :, k, :]), [full("BO")], [full("LD")], waw=(k == 0))
+    op("v", lambda e: e.memset(T.LS[:], 0.0), [], [full("LS")])
+    op("v", lambda e: e.tensor_copy(T.EV16[:], T.EVI[:]), [full("EVI")], [full("EV16")])
+    op("v", lambda e: e.tensor_copy(T.EVF[:], T.EVI[:]), [full("EVI")], [full("EVF")])
+    for z in range(4):
+        mm(T.MR3[:, z::4], T.LV[:, z, :], T.EVF[:], True, True, [("LV", 128 * z, 128 * z + 128), full("EVF")], [full("MR3")])
+
+    def ring_list(b):
+        if b == 0:
+            win, off, rd = T.RI[:], T.EU16[:, 0:32], [full("RI"), ("EU16", 0, 128)]
+        else:
+            n = V + E * b
+            win, off, rd = T.RW[:, 0:n], T["LW%d" % (b - 1)][:, 64:96], [("RW", 0, n), ("LW%d" % (b - 1), 64, 96)]
+        op("v", lambda e: e.tensor_tensor(T.XM[:], win.indirect(off), T.MK[:], A.mult), rd + [full("MK")], [full("XM")])
+        op("v", lambda e: e.tensor_tensor_scan(T.XS[:], T.RS[:], T.XM[:], 0.0, A.mult, A.add), [full("RS"), full("XM")], [full("XS")])
+        op("v", lambda e: e.tensor_copy(T["OF%d" % b][:], T.XS[:, 3::4]), [full("XS")], [full("OF%d" % b)])
+
+    def ring_diff(b):
+        op("v", lambda e: e.tensor_tensor(T.DF[:], T.VW[:, 128 * b:128 * b + 128], T.XS[:, 3::4], A.subtract),
+           [("VW", 128 * b, 128 * b + 128), full("XS")], [full("DF")])
+
+    def place_scatter(b):
+        op("v", lambda e: e.tensor_scalar(T.LL[:, 0:V].indirect(T.EU16[:, 32 * b:32 * b + 32]), T.IE[:], 1.0, float(V + E * b), A.mult, A.add),
+           [full("IE"), ("EU16", 0, 128)], [("LL", 0, V)], waw=True)
+
+    def place_next(b):
+        if b < NB - 1:
+            gath("s", T.LL[:, V:V + E], T.LL[:, 0:V], T.EU16[:, 32 * b + 32:32 * b + 64], [("LL", 0, V), ("EU16", 0, 128)], [("LL", V, V + E)])
+
+    def place_mm(b, i0, i1):
+        n = 96 if b < NB - 1 else 64
+        for i in range(i0, i1):
+            mm(T.LX[:, 0:n], T.DI[:, i, :], T.LL[:, i:16 * n:16], i == 0, i == 15, [("DI", 128 * i, 128 * i + 128), ("LL", 0, 16 * n)], [("LX", 0, n)])
+
+    def place_out(b):
+        n = 96 if b < NB - 1 else 64
+        op("v", lambda e: e.tensor_copy(T["LW%d" % b][:, 0:n], T.LX[:, 0:n]), [("LX", 0, n)], [("LW%d" % b, 0, n)])
+
+    def mem_u(b, q):
+        mu = "MU%d" % (b % 2)
+        if b == 0:
+            gath(q, T[mu][:], T.TB0[:, own:own + V], T.EU16[:, 0:32], [("TB0", own, own + V), ("EU16", 0, 128)], [full(mu)])
+        else:
+            n = V + E * b
+            gath(q, T[mu][:], T.OB[:, 0:n], T["LW%d" % (b - 1)][:, 64:96], [("OB", 0, n), ("LW%d" % (b - 1), 64, 96)], [full(mu)])
+
+    def block_half(b, h, q, dst, base):
+        n = V + E * (b + 1)
+        return gath(q, T[dst][:, base + 512 * h:base + 512 * h + 512], T.OB[:, 0:n], T["LW%d" % b][:, 32 * h:32 * h + 32],
+                    [("OB", 0, n), ("LW%d" % b, 0, 64)], [(dst, base + 512 * h, base + 512 * h + 512)])
+
+    def send_half(b, h):
+        tb = "TB%d" % (b + 1)
+        c0 = own + 512 * h
+        order("g", [(tb, c0, c0 + 512)], [])
+        ap = T[tb][:, c0:c0 + 512]
+        mask = topo.mask(core, peers[0])
+        ids = []
+        for p in peers:
+            rid, pid, _ = topo.addr(p)
+            mask &= topo.mask(core, p)
+            ids.append(DstId(rid=rid, pnc=pid))
+        ne = bin(mask).count("1")
+        g.remote_dma_fused([RemoteDMATransfer(dst_ids=ids, dma_engine_mask=mask, remote_sem=T.sem["arr%d" % b],
+                                              srcs=[ap], dsts=[ap] * len(ids))], local_sem=T.sem.sent)
+        total["sent"] = total.get("sent", 0) + ne
+        if h == 1:
+            total["arr%d" % b] = 2 * ne * len(peers)
+            rec = ("arr%d" % b, total["arr%d" % b], {})
+            for p in peers:
+                o = T.rank_of(p) * V
+                note("far", rec, [], [(tb, o, o + V)])
+
+    ring_list(0)
+    place_scatter(0)
+    place_next(0)
+    op("s", lambda e: e.activation(T.VW[:], T.MR3[:], F.Copy), [full("MR3")], [full("VW")])
+    for h in range(2):
+        op("v", lambda e: e.tensor_tensor(T.S2[:, h, :], T.LE[:, 2 * h, :], T.LE[:, 2 * h + 1, :], A.add), [full("LE")], [("S2", 128 * h, 128 * h + 128)])
+    op("v", lambda e: e.tensor_tensor(T.SK[:], T.S2[:, 0, :], T.S2[:, 1, :], A.add), [full("S2")], [full("SK")])
+    for a in range(4):
+        op("v", lambda e: e.tensor_copy(T.LS[:, a, :, a, :], T.SK[:, :, a, :]), [full("SK")], [full("LS")], waw=(a == 0))
+    ring_diff(0)
+    mem_u(0, "s")
+
+    for b in range(NB):
+        last = b == NB - 1
+        tb, mt, mu, mv = "TB%d" % b, "MT%d" % (b % 2), "MU%d" % (b % 2), "MV%d" % (b % 2)
+        place_mm(b, 0, PM[0])
+        mm(T.W[:], T.ID[:], T[mu][:], True, False, [full("ID"), full(mu)], [full("W")])
+        gath("v", T[mv][:], T[tb][:], T.EV16[:, 32 * b:32 * b + 32], [full(tb), ("EV16", 0, 128)], [full(mv)])
+        for c in range(NCH):
+            gath("s", T[mt][:, 512 * c:512 * c + 512], T[tb][:], T["OF%d" % b][:, 32 * c:32 * c + 32], [full(tb), full("OF%d" % b)], [(mt, 512 * c, 512 * c + 512)])
+        for c in range(NCH):
+            for k in range(4):
+                mm(T["MR%d" % c][:, k::4], T.ID[:], T[mv][:, 128 * c:128 * c + 128], True, True, [full("ID"), full(mv)], [full("MR%d" % c)])
+            if c == 1:
+                mm(T.W[:], T.ID[:], T[mv][:], False, True, [full("ID"), full(mv)], [full("W")])
+        place_mm(b, PM[0], PM[1])
+
+        def scan(c):
+            s = (512 * c, 512 * c + 512)
+            op("v", lambda e: e.tensor_tensor_scan(T.MX[:, s[0]:s[1]], T.RS[:], T[mt][:, s[0]:s[1]], 0.0, A.mult, A.max),
+               [full("RS"), (mt,) + s], [("MX",) + s])
+
+        def prod(c):
+            s = (512 * c, 512 * c + 512)
+            op("v", lambda e: e.tensor_tensor(T.PR[:, s[0]:s[1]], T["MR%d" % c][:], T[mt][:, s[0]:s[1]], A.mult), [full("MR%d" % c), (mt,) + s], [("PR",) + s])
+            db, d0 = ("DB", "DB", "MR0", "MR0")[c], (0, 128, 0, 128)[c]
+            for k in range(4):
+                mm(T[db][:, d0:d0 + 128], T.LD[:, k], T.PR[:, s[0] + k:s[1]:4], k == 0, k == 3, [full("LD"), ("PR",) + s], [(db, d0, d0 + 128)])
+
+        def fresh(c0, c1):
+            e0, e1 = 128 * c0, 128 * c1
+            o = V + E * b
+            op("v", lambda e: e.tensor_tensor(T.SS[:, e0:e1], T.W[:, e0:e1], T.MX[:, 4 * e0 + 3:4 * e1:4], A.subtract), [full("W"), ("MX", 4 * e0, 4 * e1)], [("SS", e0, e1)])
+            op("v", lambda e: e.tensor_scalar(T.OB[:, o + e0:o + e1], T.SS[:, e0:e1], 0.0, 15.0, A.max, A.min), [("SS", e0, e1)], [("OB", o + e0, o + e1)])
+
+        scan(0)
+        prod(0)
+        place_mm(b, PM[1], PM[2])
+        scan(1)
+        prod(1)
+        place_mm(b, PM[2], PM[3])
+        scan(2)
+        fresh(0, 3)
+        if last:
+            prod(2)
+            scan(3)
+            prod(3)
+            place_out(b)
+            fresh(3, 4)
+        else:
+            scan(3)
+            fresh(3, 4)
+            place_out(b)
+            for h in range(2):
+                block_half(b, h, "s", "TB%d" % (b + 1), own)
+                send_half(b, h)
+            prod(2)
+            prod(3)
+        for h, db in enumerate(("DB", "MR0")):
+            op("v", lambda e: e.tensor_scalar(T.SG[:, 256 * h:256 * h + 256], T[db][:, 0:256], T.CF[:, 2:3], 0.0, A.add, A.is_gt),
+               [(db, 0, 256), ("CF", 2, 3)], [("SG", 256 * h, 256 * h + 256)])
+        for a in range(4):
+            mm(T.CX[:, 0:128], T.LS[:, a], T.SG[:, a::4], a == 0, a == 3, [full("LS"), full("SG")], [("CX", 0, 128)])
+        if last:
+            for h in range(2):
+                block_half(b, h, "s", "YB", 0)
+                dmas([("y", T.ym[:, 512 * h:512 * h + 512], T.YB[:, 512 * h:512 * h + 512])], [("YB", 512 * h, 512 * h + 512)], [])
+        op("v", lambda e: e.tensor_scalar(T.MR1[:, 0:128], T.CX[:, 0:128], 3.5, None, A.is_ge), [("CX", 0, 128)], [("MR1", 0, 128)])
+        op("v", lambda e: e.tensor_tensor(T.MR1[:, 128:256], T.MR1[:, 0:128], T.DF[:], A.mult), [("MR1", 0, 128), full("DF")], [("MR1", 128, 256)])
+        op("v", lambda e: e.tensor_tensor(T.ON[:], T.MR1[:, 128:256], T.XS[:, 3::4], A.add), [("MR1", 128, 256), full("XS")], [full("ON")])
+        for a in range(4):
+            mm(T.CX[:, a::4], T.LE[:, a, :], T.ON[:], True, True, [("LE", 128 * a, 128 * a + 128), full("ON")], [full("CX")])
+        o = V + E * b
+        if b == 0:
+            op("v", lambda e: e.tensor_copy(T.RW[:, 0:V], T.RI[:]), [full("RI")], [("RW", 0, V)])
+        if not last:
+            mem_u(b + 1, "s")
+            op("s", lambda e: e.activation(T.RW[:, o:o + E], T.CX[:], F.Copy), [full("CX")], [("RW", o, o + E)])
+            place_scatter(b + 1)
+            place_next(b + 1)
+            ring_list(b + 1)
+            ring_diff(b + 1)
+        else:
+            n = V + E * NB
+            op("s", lambda e: e.activation(T.RW[:, o:o + E], T.CX[:], F.Copy), [full("CX")], [("RW", o, o + E)])
+            for h in range(2):
+                gath("vs"[h], T.YR[:, 512 * h:512 * h + 512], T.RW[:, 0:n], T.LW3[:, 32 * h:32 * h + 32], [("RW", 0, n), ("LW3", 0, 64)], [("YR", 512 * h, 512 * h + 512)])
+                dmas([("ys"[h], T.yr[k::4, 512 * h:512 * h + 512], T.YR[k::16, 512 * h:512 * h + 512]) for k in range(4)], [("YR", 512 * h, 512 * h + 512)], [])
+    for s in total:
+        if waited.get(s, 0) < total[s]:
+            g.wait_ge(T.sem[s], total[s])

@@ -2,15 +2,15 @@ from concourse.bass import DstId, RemoteDMATransfer
 from concourse.mybir import AluOpType as A, ActivationFunctionType as F
 
 NB, V, E, R = 4, 1024, 512, 4
-NCH = 4
-PM = (9, 9, 12, 16)
+PL0 = (10, 11, 13, 16)
+PL1 = (0, 0, 0, 0, 0, 4, 4, 16)
+PL = (0, 0, 3, 6, 8, 8, 8, 16)
 BF, F32, I32, U16 = "bfloat16", "float32", "int32", "uint16"
 
 SCRATCH = {
     "OB": ("sbuf", [128, V + NB * E], BF),
     "RW": ("sbuf", [128, V + NB * E], F32),
     "RI": ("sbuf", [128, V], I32),
-    "LL": ("sbuf", [128, V + E], F32),
     "IE": ("sbuf", [128, E], F32),
     "EUI": ("sbuf", [128, 128], I32), "EVI": ("sbuf", [128, 128], I32),
     "EU16": ("sbuf", [128, 128], U16), "EV16": ("sbuf", [128, 128], U16), "EVF": ("sbuf", [128, 128], F32),
@@ -22,9 +22,9 @@ SCRATCH = {
     "ONE": ("sbuf", [128, 128], BF), "ID": ("sbuf", [128, 128], BF), "IF": ("sbuf", [128, 128], F32),
     "DI": ("sbuf", [128, 16, 128], F32), "RQ": ("sbuf", [128, 16], F32), "CI": ("sbuf", [128, 16], F32),
     "LE": ("sbuf", [128, 4, 128], F32), "LV": ("sbuf", [128, 4, 128], F32),
-    "BO": ("sbuf", [128, 8, 4, 4], BF), "B1": ("sbuf", [128, 128], BF),
-    "LD": ("sbuf", [128, 4, 8, 4, 4], BF), "SK": ("sbuf", [128, 8, 4, 4], F32), "S2": ("sbuf", [128, 2, 128], F32),
-    "LS": ("sbuf", [128, 4, 8, 4, 4], BF),
+    "BO": ("sbuf", [128, 128], BF), "B1": ("sbuf", [128, 128], BF),
+    "LD": ("sbuf", [128, 4, 128], BF), "LS": ("sbuf", [128, 4, 128], BF), "CD": ("sbuf", [128, 4, 128], BF),
+    "C4": ("sbuf", [128, 12], F32), "CK": ("sbuf", [128, 4], F32),
     "Q4": ("sbuf", [128, 512], F32), "MK": ("sbuf", [128, 512], F32), "RS": ("sbuf", [128, 512], BF),
     "PC": ("sbuf", [128, 4], I32), "CF": ("sbuf", [128, 4], F32),
     "W": ("psum", [128, 512], F32), "DB": ("psum", [128, 512], F32), "CX": ("psum", [128, 512], F32), "LX": ("psum", [128, 512], F32),
@@ -35,6 +35,7 @@ for _c in range(4):
     SCRATCH["LW%d" % _c] = ("sbuf", [128, 96], U16)
     SCRATCH["MR%d" % _c] = ("psum", [128, 512], F32)
 for _c in range(2):
+    SCRATCH["LL%d" % _c] = ("sbuf", [128, V + E], F32)
     SCRATCH["MU%d" % _c] = ("sbuf", [128, 512], BF)
     SCRATCH["MV%d" % _c] = ("sbuf", [128, 512], BF)
     SCRATCH["MT%d" % _c] = ("sbuf", [128, 2048], BF)
@@ -118,6 +119,9 @@ def rank_program(g, core, T, topo):
     def mm(out, lhsT, rhs, start, stop, reads, writes):
         op("p", lambda e: e.matmul(out, lhsT, rhs, start, stop), reads, writes)
 
+    def cp(out, in_, reads, writes, scale=1.0):
+        op("s", lambda e: e.activation(out, in_, F.Copy, scale=scale), reads, writes)
+
     def gath(q, out, win, off, reads, writes):
         if q == "v":
             return op(q, lambda e: e.tensor_copy(out, win.indirect(off)), reads, writes)
@@ -132,47 +136,58 @@ def rank_program(g, core, T, topo):
     def sel(out, in_, pat, cmp, base, cm):
         return lambda e: e.affine_select(out, in_, pat, cmp, 0.0, base, cm)
 
+    def ts(out, in_, s1, s2, o0, o1, reads, writes):
+        if o1 is None:
+            op("v", lambda e: e.tensor_scalar(out, in_, s1, None, o0), reads, writes)
+        else:
+            op("v", lambda e: e.tensor_scalar(out, in_, s1, s2, o0, o1), reads, writes)
+
     one = T.ONE[:]
     op("v", lambda e: e.memset(one, 1.0), [], [full("ONE")])
     op("g", lambda e: e.iota(T.PC[:, 0:1], [[0, 1]], 0, 1), [], [("PC", 0, 1)])
     op("g", lambda e: e.iota(T.RQ[:], [[1, 16]], 0, 0, allow_small_or_imprecise_dtypes=True), [], [full("RQ")])
+    op("g", sel(T.IF[:], one, [[-1, 128]], A.is_equal, 0, 1), [full("ONE")], [full("IF")])
+    op("g", lambda e: e.iota(T.LL0[:, 0:V], [[1, V]], 0, 0, allow_small_or_imprecise_dtypes=True), [], [("LL0", 0, V)])
+    op("g", sel(T.ID[:], one, [[-1, 128]], A.is_equal, 0, 1), [full("ONE")], [full("ID")])
     op("g", sel(T.B1[:], one, [[-16, 8], [0, 16]], A.is_ge, 0, 1), [full("ONE")], [full("B1")])
     op("g", sel(T.BO[:], T.B1[:], [[16, 8], [0, 16]], A.is_ge, 15, -1), [full("B1")], [full("BO")])
-    op("g", sel(T.IF[:], one, [[-1, 128]], A.is_equal, 0, 1), [full("ONE")], [full("IF")])
-    for a in range(4):
-        op("g", sel(T.LE[:, a, :], one, [[-16, 8], [0, 4], [-1, 4]], A.is_equal, -4 * a, 1), [full("ONE")], [("LE", 128 * a, 128 * a + 128)])
-    op("g", lambda e: e.iota(T.IE[:], [[1, E]], 0, 0, allow_small_or_imprecise_dtypes=True), [], [full("IE")])
-    op("g", lambda e: e.iota(T.LL[:, 0:V], [[1, V]], 0, 0, allow_small_or_imprecise_dtypes=True), [], [("LL", 0, V)])
-    op("g", sel(T.ID[:], one, [[-1, 128]], A.is_equal, 0, 1), [full("ONE")], [full("ID")])
     for z in range(4):
         op("g", sel(T.LV[:, z, :], one, [[-16, 8], [-1, 4], [0, 4]], A.is_equal, -4 * z, 1), [full("ONE")], [("LV", 128 * z, 128 * z + 128)])
-
-    op("v", lambda e: e.tensor_scalar(T.PC[:, 1:2], T.PC[:, 0:1], 3, None, A.bitwise_and), [("PC", 0, 1)], [("PC", 1, 2)])
-    op("v", lambda e: e.tensor_scalar(T.PC[:, 2:3], T.PC[:, 0:1], 2, 3, A.logical_shift_right, A.bitwise_and), [("PC", 0, 1)], [("PC", 2, 3)])
-    op("v", lambda e: e.tensor_scalar(T.PC[:, 3:4], T.PC[:, 0:1], 15, None, A.bitwise_and), [("PC", 0, 1)], [("PC", 3, 4)])
     for a in range(4):
-        op("v", lambda e: e.memset(T.Q4[:, a::4], float(a)), [], [full("Q4")])
+        op("g", sel(T.LE[:, a, :], one, [[-16, 8], [0, 4], [-1, 4]], A.is_equal, -4 * a, 1), [full("ONE")], [("LE", 128 * a, 128 * a + 128)])
+
+    ts(T.PC[:, 3:4], T.PC[:, 0:1], 15, None, A.bitwise_and, None, [("PC", 0, 1)], [("PC", 3, 4)])
+    ts(T.PC[:, 2:3], T.PC[:, 0:1], 2, 3, A.logical_shift_right, A.bitwise_and, [("PC", 0, 1)], [("PC", 2, 3)])
     op("v", lambda e: e.tensor_copy(T.CF[:, 3:4], T.PC[:, 3:4]), [("PC", 3, 4)], [("CF", 3, 4)])
     op("v", lambda e: e.tensor_copy(T.CF[:, 0:1], T.PC[:, 2:3]), [("PC", 2, 3)], [("CF", 0, 1)])
-    op("v", lambda e: e.tensor_tensor(T.CF[:, 1:2], T.PC[:, 2:3], T.PC[:, 1:2], A.is_ge), [("PC", 1, 3)], [("CF", 1, 2)])
+    ts(T.CI[:], T.RQ[:], T.CF[:, 3:4], None, A.is_equal, None, [full("RQ"), ("CF", 3, 4)], [full("CI")])
+    for a in range(4):
+        op("v", lambda e: e.memset(T.Q4[:, a::4], float(a)), [], [full("Q4")])
     op("v", lambda e: e.memset(T.RS[:], 1.0), [], [full("RS")])
-    op("v", lambda e: e.tensor_scalar(T.CI[:], T.RQ[:], T.CF[:, 3:4], None, A.is_equal), [full("RQ"), ("CF", 3, 4)], [full("CI")])
-    op("v", lambda e: e.tensor_scalar(T.CF[:, 2:3], T.CF[:, 1:2], -0.5, None, A.add), [("CF", 1, 2)], [("CF", 2, 3)])
-    op("v", lambda e: e.tensor_scalar(T.MK[:], T.Q4[:], T.CF[:, 0:1], None, A.is_equal), [full("Q4"), ("CF", 0, 1)], [full("MK")])
+    ts(T.MK[:], T.Q4[:], T.CF[:, 0:1], None, A.is_equal, None, [full("Q4"), ("CF", 0, 1)], [full("MK")])
     op("v", lambda e: e.memset(T.RS[:, 0::4], 0.0), [], [full("RS")], waw=True)
-    op("v", lambda e: e.memset(T.LD[:], 0.0), [], [full("LD")])
     for i in range(16):
-        op("s", lambda e: e.activation(T.DI[:, i, :], T.IF[:], F.Copy, scale=T.CI[:, i:i + 1]), [full("IF"), full("CI")], [("DI", 128 * i, 128 * i + 128)])
-    for k in range(4):
-        op("v", lambda e: e.tensor_scalar(T.LD[:, k, :, :, k], T.BO[:, :, :, k], -1.0, None, A.mult), [full("BO")], [full("LD")], waw=(k == 0))
+        cp(T.DI[:, i, :], T.IF[:], [full("IF"), full("CI")], [("DI", 128 * i, 128 * i + 128)], scale=T.CI[:, i:i + 1])
     op("v", lambda e: e.tensor_copy(T.EU16[:], T.EUI[:]), [full("EUI")], [full("EU16")])
-    for k in range(4):
-        op("v", lambda e: e.tensor_copy(T.LD[:, k, :, k, :], T.BO[:, :, k, :]), [full("BO")], [full("LD")], waw=(k == 0))
-    op("v", lambda e: e.memset(T.LS[:], 0.0), [], [full("LS")])
+    ts(T.PC[:, 1:2], T.PC[:, 0:1], 3, None, A.bitwise_and, None, [("PC", 0, 1)], [("PC", 1, 2)])
     op("v", lambda e: e.tensor_copy(T.EV16[:], T.EVI[:]), [full("EVI")], [full("EV16")])
+    op("v", lambda e: e.tensor_tensor(T.CF[:, 1:2], T.PC[:, 2:3], T.PC[:, 1:2], A.is_ge), [("PC", 1, 3)], [("CF", 1, 2)])
+    ts(T.CF[:, 2:3], T.CF[:, 1:2], -0.5, None, A.add, None, [("CF", 1, 2)], [("CF", 2, 3)])
+    op("v", lambda e: e.tensor_copy(T.C4[:, 11:12], T.PC[:, 1:2]), [("PC", 1, 2)], [("C4", 11, 12)])
+    ts(T.C4[:, 0:4], T.RQ[:, 0:4], T.CF[:, 0:1], None, A.is_equal, None, [full("RQ"), ("CF", 0, 1)], [("C4", 0, 4)])
+    ts(T.C4[:, 4:8], T.RQ[:, 0:4], T.C4[:, 11:12], None, A.is_equal, None, [full("RQ"), ("C4", 11, 12)], [("C4", 4, 8)])
+    op("v", lambda e: e.tensor_tensor(T.CK[:], T.C4[:, 0:4], T.C4[:, 4:8], A.subtract), [("C4", 0, 8)], [full("CK")])
     op("v", lambda e: e.tensor_copy(T.EVF[:], T.EVI[:]), [full("EVI")], [full("EVF")])
+    cp(T.IE[:], T.LL0[:, 0:E], [("LL0", 0, E)], [full("IE")])
+    for k in range(4):
+        cp(T.CD[:, k, :], T.ID[:], [full("ID"), full("CK")], [("CD", 128 * k, 128 * k + 128)], scale=T.CK[:, k:k + 1])
+    mm(T.DB[:], T.BO[:], T.CD[:], True, True, [full("BO"), full("CD")], [full("DB")])
+    cp(T.LD[:], T.DB[:], [full("DB")], [full("LD")])
     for z in range(4):
         mm(T.MR3[:, z::4], T.LV[:, z, :], T.EVF[:], True, True, [("LV", 128 * z, 128 * z + 128), full("EVF")], [full("MR3")])
+    cp(T.VW[:], T.MR3[:], [full("MR3")], [full("VW")])
+    for a in range(4):
+        mm(T.CX[:, 128 * a:128 * a + 128], T.LE[:, a, :], T.IF[:], True, True, [("LE", 128 * a, 128 * a + 128), full("IF")], [full("CX")])
 
     def ring_list(b):
         if b == 0:
@@ -189,29 +204,33 @@ def rank_program(g, core, T, topo):
            [("VW", 128 * b, 128 * b + 128), full("XS")], [full("DF")])
 
     def place_scatter(b):
-        op("v", lambda e: e.tensor_scalar(T.LL[:, 0:V].indirect(T.EU16[:, 32 * b:32 * b + 32]), T.IE[:], 1.0, float(V + E * b), A.mult, A.add),
-           [full("IE"), ("EU16", 0, 128)], [("LL", 0, V)], waw=True)
+        ll = "LL%d" % (b % 2)
+        op("v", lambda e: e.tensor_scalar(T[ll][:, 0:V].indirect(T.EU16[:, 32 * b:32 * b + 32]), T.IE[:], 1.0, float(V + E * b), A.mult, A.add),
+           [full("IE"), ("EU16", 0, 128)], [(ll, 0, V)], waw=True)
 
     def place_next(b):
+        ll = "LL%d" % (b % 2)
         if b < NB - 1:
-            gath("s", T.LL[:, V:V + E], T.LL[:, 0:V], T.EU16[:, 32 * b + 32:32 * b + 64], [("LL", 0, V), ("EU16", 0, 128)], [("LL", V, V + E)])
+            gath("s", T[ll][:, V:V + E], T[ll][:, 0:V], T.EU16[:, 32 * b + 32:32 * b + 64], [(ll, 0, V), ("EU16", 0, 128)], [(ll, V, V + E)])
 
     def place_mm(b, i0, i1):
-        n = 96 if b < NB - 1 else 64
+        if b >= NB:
+            return
+        n, ll = 96 if b < NB - 1 else 64, "LL%d" % (b % 2)
         for i in range(i0, i1):
-            mm(T.LX[:, 0:n], T.DI[:, i, :], T.LL[:, i:16 * n:16], i == 0, i == 15, [("DI", 128 * i, 128 * i + 128), ("LL", 0, 16 * n)], [("LX", 0, n)])
+            mm(T.LX[:, 0:n], T.DI[:, i, :], T[ll][:, i:16 * n:16], i == 0, i == 15, [("DI", 128 * i, 128 * i + 128), (ll, 0, 16 * n)], [("LX", 0, n)])
 
     def place_out(b):
         n = 96 if b < NB - 1 else 64
         op("v", lambda e: e.tensor_copy(T["LW%d" % b][:, 0:n], T.LX[:, 0:n]), [("LX", 0, n)], [("LW%d" % b, 0, n)])
 
-    def mem_u(b, q):
+    def mem_u(b):
         mu = "MU%d" % (b % 2)
         if b == 0:
-            gath(q, T[mu][:], T.TB0[:, own:own + V], T.EU16[:, 0:32], [("TB0", own, own + V), ("EU16", 0, 128)], [full(mu)])
+            gath("s", T[mu][:], T.TB0[:, own:own + V], T.EU16[:, 0:32], [("TB0", own, own + V), ("EU16", 0, 128)], [full(mu)])
         else:
             n = V + E * b
-            gath(q, T[mu][:], T.OB[:, 0:n], T["LW%d" % (b - 1)][:, 64:96], [("OB", 0, n), ("LW%d" % (b - 1), 64, 96)], [full(mu)])
+            gath("s", T[mu][:], T.OB[:, 0:n], T["LW%d" % (b - 1)][:, 64:96], [("OB", 0, n), ("LW%d" % (b - 1), 64, 96)], [full(mu)])
 
     def block_half(b, h, q, dst, base):
         n = V + E * (b + 1)
@@ -242,30 +261,20 @@ def rank_program(g, core, T, topo):
 
     ring_list(0)
     place_scatter(0)
+    cp(T.LL1[:, 0:V], T.LL0[:, 0:V], [("LL0", 0, V)], [("LL1", 0, V)])
     place_next(0)
-    op("s", lambda e: e.activation(T.VW[:], T.MR3[:], F.Copy), [full("MR3")], [full("VW")])
-    for h in range(2):
-        op("v", lambda e: e.tensor_tensor(T.S2[:, h, :], T.LE[:, 2 * h, :], T.LE[:, 2 * h + 1, :], A.add), [full("LE")], [("S2", 128 * h, 128 * h + 128)])
-    op("v", lambda e: e.tensor_tensor(T.SK[:], T.S2[:, 0, :], T.S2[:, 1, :], A.add), [full("S2")], [full("SK")])
-    for a in range(4):
-        op("v", lambda e: e.tensor_copy(T.LS[:, a, :, a, :], T.SK[:, :, a, :]), [full("SK")], [full("LS")], waw=(a == 0))
-    ring_diff(0)
-    mem_u(0, "s")
+    op("v", lambda e: e.tensor_copy(T.RW[:, 0:V], T.RI[:]), [full("RI")], [("RW", 0, V)])
+    place_scatter(1)
+    mem_u(0)
+    place_mm(0, 0, PL0[0])
 
     for b in range(NB):
         last = b == NB - 1
         tb, mt, mu, mv = "TB%d" % b, "MT%d" % (b % 2), "MU%d" % (b % 2), "MV%d" % (b % 2)
-        place_mm(b, 0, PM[0])
-        mm(T.W[:], T.ID[:], T[mu][:], True, False, [full("ID"), full(mu)], [full("W")])
-        gath("v", T[mv][:], T[tb][:], T.EV16[:, 32 * b:32 * b + 32], [full(tb), ("EV16", 0, 128)], [full(mv)])
-        for c in range(NCH):
-            gath("s", T[mt][:, 512 * c:512 * c + 512], T[tb][:], T["OF%d" % b][:, 32 * c:32 * c + 32], [full(tb), full("OF%d" % b)], [(mt, 512 * c, 512 * c + 512)])
-        for c in range(NCH):
-            for k in range(4):
-                mm(T["MR%d" % c][:, k::4], T.ID[:], T[mv][:, 128 * c:128 * c + 128], True, True, [full("ID"), full(mv)], [full("MR%d" % c)])
-            if c == 1:
-                mm(T.W[:], T.ID[:], T[mv][:], False, True, [full("ID"), full(mv)], [full("W")])
-        place_mm(b, PM[0], PM[1])
+        pl = PL1 if b == 0 else PL
+
+        def lmm(j):
+            place_mm(b + 1, pl[j], pl[j + 1])
 
         def scan(c):
             s = (512 * c, 512 * c + 512)
@@ -277,67 +286,118 @@ def rank_program(g, core, T, topo):
             op("v", lambda e: e.tensor_tensor(T.PR[:, s[0]:s[1]], T["MR%d" % c][:], T[mt][:, s[0]:s[1]], A.mult), [full("MR%d" % c), (mt,) + s], [("PR",) + s])
             db, d0 = ("DB", "DB", "MR0", "MR0")[c], (0, 128, 0, 128)[c]
             for k in range(4):
-                mm(T[db][:, d0:d0 + 128], T.LD[:, k], T.PR[:, s[0] + k:s[1]:4], k == 0, k == 3, [full("LD"), ("PR",) + s], [(db, d0, d0 + 128)])
+                mm(T[db][:, d0:d0 + 128], T.LD[:, k, :], T.PR[:, s[0] + k:s[1]:4], k == 0, k == 3, [full("LD"), ("PR",) + s], [(db, d0, d0 + 128)])
 
-        def fresh(c0, c1):
+        def sub(c0, c1):
+            e0, e1 = 128 * c0, 128 * c1
+            op("v", lambda e: e.tensor_tensor(T.SS[:, e0:e1], T.W[:, e0:e1], T.MX[:, 4 * e0 + 3:4 * e1:4], A.subtract), [full("W"), ("MX", 4 * e0, 4 * e1)], [("SS", e0, e1)])
+
+        def clip(c0, c1):
             e0, e1 = 128 * c0, 128 * c1
             o = V + E * b
-            op("v", lambda e: e.tensor_tensor(T.SS[:, e0:e1], T.W[:, e0:e1], T.MX[:, 4 * e0 + 3:4 * e1:4], A.subtract), [full("W"), ("MX", 4 * e0, 4 * e1)], [("SS", e0, e1)])
-            op("v", lambda e: e.tensor_scalar(T.OB[:, o + e0:o + e1], T.SS[:, e0:e1], 0.0, 15.0, A.max, A.min), [("SS", e0, e1)], [("OB", o + e0, o + e1)])
+            ts(T.OB[:, o + e0:o + e1], T.SS[:, e0:e1], 0.0, 15.0, A.max, A.min, [("SS", e0, e1)], [("OB", o + e0, o + e1)])
 
-        scan(0)
-        prod(0)
-        place_mm(b, PM[1], PM[2])
-        scan(1)
-        prod(1)
-        place_mm(b, PM[2], PM[3])
-        scan(2)
-        fresh(0, 3)
-        if last:
-            prod(2)
-            scan(3)
-            prod(3)
-            place_out(b)
-            fresh(3, 4)
-        else:
-            scan(3)
-            fresh(3, 4)
-            place_out(b)
-            for h in range(2):
-                block_half(b, h, "s", "TB%d" % (b + 1), own)
-                send_half(b, h)
-            prod(2)
-            prod(3)
-        for h, db in enumerate(("DB", "MR0")):
-            op("v", lambda e: e.tensor_scalar(T.SG[:, 256 * h:256 * h + 256], T[db][:, 0:256], T.CF[:, 2:3], 0.0, A.add, A.is_gt),
-               [(db, 0, 256), ("CF", 2, 3)], [("SG", 256 * h, 256 * h + 256)])
-        for a in range(4):
-            mm(T.CX[:, 0:128], T.LS[:, a], T.SG[:, a::4], a == 0, a == 3, [full("LS"), full("SG")], [("CX", 0, 128)])
-        if last:
-            for h in range(2):
-                block_half(b, h, "s", "YB", 0)
-                dmas([("y", T.ym[:, 512 * h:512 * h + 512], T.YB[:, 512 * h:512 * h + 512])], [("YB", 512 * h, 512 * h + 512)], [])
-        op("v", lambda e: e.tensor_scalar(T.MR1[:, 0:128], T.CX[:, 0:128], 3.5, None, A.is_ge), [("CX", 0, 128)], [("MR1", 0, 128)])
-        op("v", lambda e: e.tensor_tensor(T.MR1[:, 128:256], T.MR1[:, 0:128], T.DF[:], A.mult), [("MR1", 0, 128), full("DF")], [("MR1", 128, 256)])
-        op("v", lambda e: e.tensor_tensor(T.ON[:], T.MR1[:, 128:256], T.XS[:, 3::4], A.add), [("MR1", 128, 256), full("XS")], [full("ON")])
-        for a in range(4):
-            mm(T.CX[:, a::4], T.LE[:, a, :], T.ON[:], True, True, [("LE", 128 * a, 128 * a + 128), full("ON")], [full("CX")])
-        o = V + E * b
+        def lowest(h):
+            db, cx = ("DB", "MR0")[h], ("CX", "MR2")[h]
+            ts(T.SG[:, 256 * h:256 * h + 256], T[db][:, 0:256], T.CF[:, 2:3], 0.0, A.add, A.is_gt, [(db, 0, 256), ("CF", 2, 3)], [("SG", 256 * h, 256 * h + 256)])
+            for a in range(4):
+                mm(T[cx][:, 0:64], T.LS[:, a, :], T.SG[:, 256 * h + a:256 * h + 256:4], a == 0, a == 3, [full("LS"), ("SG", 256 * h, 256 * h + 256)], [(cx, 0, 64)])
+
+        def pick(h):
+            cx = ("CX", "MR2")[h]
+            c0, c1, t = 64 * h, 64 * h + 64, 128 * h
+            ts(T.MR1[:, t:t + 64], T[cx][:, 0:64], 3.5, None, A.is_ge, None, [(cx, 0, 64)], [("MR1", t, t + 64)])
+            op("v", lambda e: e.tensor_tensor(T.MR1[:, t + 64:t + 128], T.MR1[:, t:t + 64], T.DF[:, c0:c1], A.mult), [("MR1", t, t + 64), full("DF")], [("MR1", t + 64, t + 128)])
+            op("v", lambda e: e.tensor_tensor(T.ON[:, c0:c1], T.MR1[:, t + 64:t + 128], T.XS[:, 256 * h + 3:256 * h + 256:4], A.add), [("MR1", t + 64, t + 128), full("XS")], [("ON", c0, c1)])
+
+        def renew(h):
+            ex, c0, c1 = ("CX", "MR3")[h], 64 * h, 64 * h + 64
+            for a in range(4):
+                mm(T[ex][:, a:256:4], T.LE[:, a, :], T.ON[:, c0:c1], True, True, [("LE", 128 * a, 128 * a + 128), ("ON", c0, c1)], [(ex, 0, 256)])
+            o = V + E * b + 256 * h
+            cp(T.RW[:, o:o + 256], T[ex][:, 0:256], [(ex, 0, 256)], [("RW", o, o + 256)])
+
+        mm(T.W[:], T.ID[:], T[mu][:], True, False, [full("ID"), full(mu)], [full("W")])
+        gath("s", T[mv][:], T[tb][:], T.EV16[:, 32 * b:32 * b + 32], [full(tb), ("EV16", 0, 128)], [full(mv)])
+        for c in range(4):
+            gath("v" if c == 0 else "s", T[mt][:, 512 * c:512 * c + 512], T[tb][:], T["OF%d" % b][:, 32 * c:32 * c + 32], [full(tb), full("OF%d" % b)], [(mt, 512 * c, 512 * c + 512)])
+        for c in range(4):
+            for k in range(4):
+                mm(T["MR%d" % c][:, k::4], T.ID[:], T[mv][:, 128 * c:128 * c + 128], True, True, [full("ID"), full(mv)], [full("MR%d" % c)])
+            if c == 1:
+                mm(T.W[:], T.ID[:], T[mv][:], False, True, [full("ID"), full(mv)], [full("W")])
         if b == 0:
-            op("v", lambda e: e.tensor_copy(T.RW[:, 0:V], T.RI[:]), [full("RI")], [("RW", 0, V)])
-        if not last:
-            mem_u(b + 1, "s")
-            op("s", lambda e: e.activation(T.RW[:, o:o + E], T.CX[:], F.Copy), [full("CX")], [("RW", o, o + E)])
-            place_scatter(b + 1)
-            place_next(b + 1)
-            ring_list(b + 1)
-            ring_diff(b + 1)
+            place_next(1)
+            cp(T.LS[:], T.CX[:], [full("CX")], [full("LS")])
+            place_mm(0, PL0[0], PL0[1])
         else:
+            place_out(b)
+        if last:
+            scan(0)
+            prod(0)
+            prod(1)
+            scan(1)
+            prod(2)
+            prod(3)
+            lowest(0)
+            ring_diff(b)
+            scan(2)
+            lowest(1)
+            pick(0)
+            renew(0)
+            pick(1)
+            renew(1)
+            scan(3)
+            sub(0, 4)
+            clip(0, 4)
             n = V + E * NB
-            op("s", lambda e: e.activation(T.RW[:, o:o + E], T.CX[:], F.Copy), [full("CX")], [("RW", o, o + E)])
             for h in range(2):
                 gath("vs"[h], T.YR[:, 512 * h:512 * h + 512], T.RW[:, 0:n], T.LW3[:, 32 * h:32 * h + 32], [("RW", 0, n), ("LW3", 0, 64)], [("YR", 512 * h, 512 * h + 512)])
                 dmas([("ys"[h], T.yr[k::4, 512 * h:512 * h + 512], T.YR[k::16, 512 * h:512 * h + 512]) for k in range(4)], [("YR", 512 * h, 512 * h + 512)], [])
+            for h in range(2):
+                block_half(b, h, "sv"[h], "YB", 0)
+                dmas([("y", T.ym[:, 512 * h:512 * h + 512], T.YB[:, 512 * h:512 * h + 512])], [("YB", 512 * h, 512 * h + 512)], [])
+            continue
+        scan(0)
+        for c in range(1, 4):
+            if c < 3:
+                prod(c - 1)
+            if b == 0 and c < 3:
+                place_mm(0, PL0[c], PL0[c + 1])
+            else:
+                lmm(c)
+            if c < 3:
+                scan(c)
+        sub(0, 3)
+        scan(3)
+        clip(0, 3)
+        if b + 2 < NB:
+            dst, src = "LL%d" % (b % 2), "LL%d" % ((b + 1) % 2)
+            dmas([("y", T[dst][:, 0:V], T[src][:, 0:V])], [(src, 0, V)], [(dst, 0, V)])
+        sub(3, 4)
+        clip(3, 4)
+        if b == 0:
+            place_out(0)
+        for h in range(2):
+            block_half(b, h, "s", "TB%d" % (b + 1), own)
+            send_half(b, h)
+        mem_u(b + 1)
+        lowest(0)
+        lmm(4)
+        prod(2)
+        prod(3)
+        ring_diff(b)
+        lmm(5)
+        lowest(1)
+        pick(0)
+        renew(0)
+        pick(1)
+        renew(1)
+        lmm(6)
+        if b + 2 < NB:
+            place_scatter(b + 2)
+            place_next(b + 2)
+        ring_list(b + 1)
     for s in total:
         if waited.get(s, 0) < total[s]:
             g.wait_ge(T.sem[s], total[s])

@@ -2,44 +2,42 @@ from concourse.bass import DstId, RemoteDMATransfer
 from concourse.mybir import AluOpType as A, ActivationFunctionType as F
 
 NB, V, E, R = 4, 1024, 512, 4
-PL0 = (10, 11, 13, 16)
-PL1 = (0, 0, 0, 0, 0, 4, 4, 16)
-PL = (0, 0, 3, 6, 8, 8, 8, 16)
 BF, F32, I32, U16 = "bfloat16", "float32", "int32", "uint16"
+LAG, FAR, SLACK = 0.12, 3.7, 0.03
 
 SCRATCH = {
     "OB": ("sbuf", [128, V + NB * E], BF),
     "RW": ("sbuf", [128, V + NB * E], F32),
     "RI": ("sbuf", [128, V], I32),
-    "IE": ("sbuf", [128, E], F32),
     "EUI": ("sbuf", [128, 128], I32), "EVI": ("sbuf", [128, 128], I32),
     "EU16": ("sbuf", [128, 128], U16), "EV16": ("sbuf", [128, 128], U16), "EVF": ("sbuf", [128, 128], F32),
-    "MX": ("sbuf", [128, 2048], BF), "PR": ("sbuf", [128, 2048], BF),
-    "SS": ("sbuf", [128, 512], BF), "SG": ("sbuf", [128, 512], BF), "ON": ("sbuf", [128, 128], F32),
-    "XM": ("sbuf", [128, 512], F32), "XS": ("sbuf", [128, 512], F32), "DF": ("sbuf", [128, 128], F32),
+    "MX": ("sbuf", [128, 2048], BF), "PR": ("sbuf", [128, 1536], BF),
+    "SG": ("sbuf", [128, 512], BF), "ON": ("sbuf", [128, 128], F32),
+    "GR": ("sbuf", [128, 512], F32), "DF": ("sbuf", [128, 128], F32),
     "VW": ("sbuf", [128, 512], F32),
     "YB": ("sbuf", [128, V], BF), "YR": ("sbuf", [128, V], F32),
-    "ONE": ("sbuf", [128, 128], BF), "ID": ("sbuf", [128, 128], BF), "IF": ("sbuf", [128, 128], F32),
-    "DI": ("sbuf", [128, 16, 128], F32), "RQ": ("sbuf", [128, 16], F32), "CI": ("sbuf", [128, 16], F32),
-    "LE": ("sbuf", [128, 4, 128], F32), "LV": ("sbuf", [128, 4, 128], F32),
+    "ONE": ("sbuf", [128, 144], BF), "ID": ("sbuf", [128, 128], BF), "NI": ("sbuf", [128, 128], BF), "IF": ("sbuf", [128, 128], F32),
+    "ZL": ("sbuf", [128, 144], BF), "ZB": ("sbuf", [128, 144], BF), "RQ": ("sbuf", [128, 16], F32), "QH": ("sbuf", [128, 16], F32),
+    "LO": ("sbuf", [128, 256], BF), "PZ": ("sbuf", [128, NB * E], BF),
+    "LE": ("sbuf", [128, 4, 128], F32), "LV": ("sbuf", [128, 4, 128], F32), "RD": ("sbuf", [128, 4, 128], F32),
     "BO": ("sbuf", [128, 128], BF), "B1": ("sbuf", [128, 128], BF),
-    "LD": ("sbuf", [128, 4, 128], BF), "LS": ("sbuf", [128, 4, 128], BF), "CD": ("sbuf", [128, 4, 128], BF),
+    "LD": ("sbuf", [128, 3, 128], BF), "LS": ("sbuf", [128, 4, 128], BF), "CD": ("sbuf", [128, 3, 128], BF),
     "C4": ("sbuf", [128, 12], F32), "CK": ("sbuf", [128, 4], F32),
-    "Q4": ("sbuf", [128, 512], F32), "MK": ("sbuf", [128, 512], F32), "RS": ("sbuf", [128, 512], BF),
-    "PC": ("sbuf", [128, 4], I32), "CF": ("sbuf", [128, 4], F32),
-    "W": ("psum", [128, 512], F32), "DB": ("psum", [128, 512], F32), "CX": ("psum", [128, 512], F32), "LX": ("psum", [128, 512], F32),
+    "RS": ("sbuf", [128, 1024], BF),
+    "PC": ("sbuf", [128, 8], I32), "CF": ("sbuf", [128, 8], F32),
+    "W0": ("psum", [128, 512], F32), "W1": ("psum", [128, 512], F32), "LX": ("psum", [128, 512], F32), "LN": ("psum", [128, 512], F32),
+    "DA0": ("psum", [128, 512], F32), "DA1": ("psum", [128, 512], F32), "CX0": ("psum", [128, 512], F32), "CX1": ("psum", [128, 512], F32),
 }
 for _c in range(4):
     SCRATCH["TB%d" % _c] = ("sbuf", [128, 4 * V], BF)
     SCRATCH["OF%d" % _c] = ("sbuf", [128, 128], U16)
     SCRATCH["LW%d" % _c] = ("sbuf", [128, 96], U16)
-    SCRATCH["MR%d" % _c] = ("psum", [128, 512], F32)
+    SCRATCH["LL%d" % _c] = ("sbuf", [128, V + E], BF)
 for _c in range(2):
-    SCRATCH["LL%d" % _c] = ("sbuf", [128, V + E], F32)
     SCRATCH["MU%d" % _c] = ("sbuf", [128, 512], BF)
     SCRATCH["MV%d" % _c] = ("sbuf", [128, 512], BF)
     SCRATCH["MT%d" % _c] = ("sbuf", [128, 2048], BF)
-NDMA = 24
+NDMA = 20
 SEMAPHORES = ["cv", "cs", "cp", "cg", "sent"] + ["arr%d" % b for b in range(NB)] + ["d%d" % i for i in range(NDMA)]
 
 
@@ -51,7 +49,8 @@ def rank_program(g, core, T, topo):
     own = rank * V
     QU = {"v": g.vector, "s": g.scalar, "p": g.tensor, "g": g, "y": g.sync}
     known = {q: {} for q in QU}
-    total, waited, acc, ndma = {}, {}, {}, [0]
+    hold, marks, prog = [None], {}, []
+    total, waited, acc, ndma, clks = {}, {}, {}, [0], {}
     psum = {n for n in SCRATCH if SCRATCH[n][0] == "psum"}
 
     def wait(q, rec):
@@ -89,26 +88,100 @@ def rank_program(g, core, T, topo):
                     lst[:] = [x for x in lst if not (c0 <= x[2] and x[3] <= c1)]
                 lst.append((q, w, c0, c1, rec))
 
-    def op(q, fn, reads, writes, waw=False):
-        order(q, reads, writes, waw=waw)
-        sem = "c" + q
-        fn(QU[q]).then_inc(T.sem[sem], 1)
-        total[sem] = total.get(sem, 0) + 1
-        rec = (sem, total[sem], dict(known[q]))
-        note(q, rec, reads, writes)
-        return rec
+    def emit(k):
+        q, reads, writes = k["q"], k["reads"], k["writes"]
+        if k["kind"] == "op":
+            order(q, reads, writes, waw=k["waw"])
+            sem = "c" + q
+            k["fn"](QU[q]).then_inc(T.sem[sem], 1)
+            total[sem] = total.get(sem, 0) + 1
+            note(q, (sem, total[sem], dict(known[q])), reads, writes)
+        elif k["kind"] == "dma":
+            order(q, reads, writes, dma=True)
+            QU[q].dma_start(*k["fn"]).then_inc(T.sem[k["sem"]], 16)
+            total[k["sem"]] = 16 * k["n"]
+            clk = clks.setdefault(k["sem"], [0, {}])
+            for s, x in known[q].items():
+                clk[1][s] = max(clk[1].get(s, 0), x)
+            clk[0] += 1
+            if clk[0] == k["n"]:
+                note("dma" + k["sem"], (k["sem"], total[k["sem"]], clk[1]), reads, writes)
+        else:
+            if k["kind"] == "send":
+                order("g", reads, [])
+            k["fn"]()
 
-    def dmas(parts, reads, writes):
+    def item(**k):
+        k["hold"] = hold[0]
+        prog.append(k)
+
+    def here():
+        return len(prog) - 1
+
+    def op(q, fn, reads, writes, waw=False, n=128, t=None):
+        item(q=q, kind="op", fn=fn, reads=reads, writes=writes, waw=waw, time=t or (0.38 if q == "g" else 0.055 + 0.00083 * max(n, 64)), lag=LAG)
+
+    def dmas(parts, reads, writes, lag=2.2):
         sem = "d%d" % ndma[0]
         ndma[0] += 1
-        clk = {}
         for q, out, in_ in parts:
-            order(q, reads, writes, dma=True)
-            QU[q].dma_start(out, in_).then_inc(T.sem[sem], 16)
-            for s, x in known[q].items():
-                clk[s] = max(clk.get(s, 0), x)
-        total[sem] = 16 * len(parts)
-        note("dma" + sem, (sem, total[sem], clk), reads, writes)
+            item(q=q, kind="dma", fn=(out, in_), reads=reads, writes=writes, time=0.06, lag=lag, sem=sem, n=len(parts))
+
+    def plan():
+        n = len(prog)
+        after, then = [set() for _ in range(n)], [[] for _ in range(n)]
+        seen, bank = {}, {}
+        for j, k in enumerate(prog):
+            regs = [(0,) + r for r in k["reads"]] + [(1,) + r for r in k["writes"]]
+            if k["hold"] is not None and prog[k["hold"]]["q"] == k["q"]:
+                after[j].add(k["hold"])
+            for w, b, c0, c1 in regs:
+                if b in psum:
+                    if bank.get(b, j) != j:
+                        after[j].add(bank[b])
+                    continue
+                for (i, w2, a0, a1) in seen.get(b, []):
+                    together = k["kind"] == prog[i]["kind"] == "dma" and k["sem"] == prog[i]["sem"]
+                    if i != j and (w or w2) and a1 > c0 and c1 > a0 and not together:
+                        after[j].add(i)
+            for w, b, c0, c1 in regs:
+                if b in psum:
+                    bank[b] = j
+                else:
+                    seen.setdefault(b, []).append((j, w, c0, c1))
+        for j in range(n):
+            for i in after[j]:
+                then[i].append(j)
+        near = lambda i, j: prog[i]["q"] == prog[j]["q"] == "p"
+        way = [0.0] * n
+        for j in range(n - 1, -1, -1):
+            k = prog[j]
+            for i in then[j]:
+                way[j] = max(way[j], way[i] - (k["lag"] if near(i, j) else 0))
+            way[j] += k["time"] + k["lag"]
+        for j in range(n):
+            way[j] += 1000.0 - j if prog[j]["kind"] == "dma" else 0.0
+        left = [len(after[j]) for j in range(n)]
+        ready = {j for j in range(n) if not left[j]}
+        at, start, free = [0.0] * n, {}, {}
+        while ready:
+            best = None
+            for j in ready:
+                t = max(at[j], free.get(prog[j]["q"], 0.0))
+                c = (t - SLACK * way[j], -way[j], j, t)
+                if best is None or c < best:
+                    best = c
+            j, t = best[2], best[3]
+            k = prog[j]
+            start[j] = t
+            free[k["q"]] = t + k["time"]
+            ready.discard(j)
+            for i in then[j]:
+                at[i] = max(at[i], t + k["time"] + (0 if near(i, j) else k["lag"]))
+                left[i] -= 1
+                if not left[i]:
+                    ready.add(i)
+        return sorted(range(n), key=lambda j: (start[j], j))
 
     def full(n):
         c = 1
@@ -116,39 +189,48 @@ def rank_program(g, core, T, topo):
             c *= d
         return (n, 0, c)
 
-    def mm(out, lhsT, rhs, start, stop, reads, writes):
-        op("p", lambda e: e.matmul(out, lhsT, rhs, start, stop), reads, writes)
+    def mm(out, lhsT, rhs, start, stop, reads, writes, n=128):
+        op("p", lambda e: e.matmul(out, lhsT, rhs, start, stop), reads, writes, t=0.04 + 0.000417 * max(n, 64))
 
-    def cp(out, in_, reads, writes, scale=1.0):
-        op("s", lambda e: e.activation(out, in_, F.Copy, scale=scale), reads, writes)
+    def cp(out, in_, reads, writes, scale=1.0, n=128):
+        op("s", lambda e: e.activation(out, in_, F.Copy, scale=scale), reads, writes, n=n)
 
     def gath(q, out, win, off, reads, writes):
+        t = 0.06 + 0.0014 * (writes[0][2] - writes[0][1])
         if q == "v":
-            return op(q, lambda e: e.tensor_copy(out, win.indirect(off)), reads, writes)
-        return op(q, lambda e: e.activation(out, win.indirect(off), F.Copy), reads, writes)
+            return op(q, lambda e: e.tensor_copy(out, win.indirect(off)), reads, writes, t=t)
+        return op(q, lambda e: e.activation(out, win.indirect(off), F.Copy), reads, writes, t=t)
 
-    dmas([("y", T.EUI[:], T.eu[:])], [], [full("EUI")])
-    dmas([("s", T.EVI[:], T.ev[:])], [], [full("EVI")])
-    dmas([("sy"[i % 2], T.RI[i::16, :], T.ring0[i % 4::4, :]) for i in range(16)], [], [full("RI")])
-    dmas([("sy"[i % 2], T.TB0[:, i * V:(i + 1) * V], T.m0[:, i * V:(i + 1) * V]) for i in range(4)], [], [full("TB0")])
-    dmas([("y", T.OB[:, 0:V], T.m0[:, own:own + V])], [], [("OB", 0, V)])
+    def sel(out, in_, pat, cmp, base, cm, fill=0.0):
+        return lambda e: e.affine_select(out, in_, pat, cmp, fill, base, cm)
 
-    def sel(out, in_, pat, cmp, base, cm):
-        return lambda e: e.affine_select(out, in_, pat, cmp, 0.0, base, cm)
-
-    def ts(out, in_, s1, s2, o0, o1, reads, writes):
+    def ts(out, in_, s1, s2, o0, o1, reads, writes, n=64):
         if o1 is None:
-            op("v", lambda e: e.tensor_scalar(out, in_, s1, None, o0), reads, writes)
+            op("v", lambda e: e.tensor_scalar(out, in_, s1, None, o0), reads, writes, n=n)
         else:
-            op("v", lambda e: e.tensor_scalar(out, in_, s1, s2, o0, o1), reads, writes)
+            op("v", lambda e: e.tensor_scalar(out, in_, s1, s2, o0, o1), reads, writes, n=n)
 
-    one = T.ONE[:]
-    op("v", lambda e: e.memset(one, 1.0), [], [full("ONE")])
+    def tt(out, x, y, o, reads, writes, n=64):
+        op("v", lambda e: e.tensor_tensor(out, x, y, o), reads, writes, n=n)
+
+    def tc(out, in_, reads, writes, n=64):
+        op("v", lambda e: e.tensor_copy(out, in_), reads, writes, n=n)
+
+    dmas([("y", T.EUI[:], T.eu[:])], [], [full("EUI")], 2.0)
+    dmas([("s", T.EVI[:], T.ev[:])], [], [full("EVI")], 2.0)
+    dmas([("sy"[i % 2], T.RI[i::16, :], T.ring0[i % 4::4, :]) for i in range(16)], [], [full("RI")], 3.7)
+    dmas([("y", T.TB0[:, own:own + V], T.m0[:, own:own + V])], [], [("TB0", own, own + V)], 4.8)
+    rest = [T.rank_of(p) * V for p in peers]
+    dmas([("s", T.TB0[:, o:o + V], T.m0[:, o:o + V]) for o in rest], [], [("TB0", o, o + V) for o in rest], 6.6)
+
+    one = T.ONE[:, 0:128]
+    op("v", lambda e: e.memset(T.ONE[:], 1.0), [], [full("ONE")])
     op("g", lambda e: e.iota(T.PC[:, 0:1], [[0, 1]], 0, 1), [], [("PC", 0, 1)])
     op("g", lambda e: e.iota(T.RQ[:], [[1, 16]], 0, 0, allow_small_or_imprecise_dtypes=True), [], [full("RQ")])
-    op("g", sel(T.IF[:], one, [[-1, 128]], A.is_equal, 0, 1), [full("ONE")], [full("IF")])
-    op("g", lambda e: e.iota(T.LL0[:, 0:V], [[1, V]], 0, 0, allow_small_or_imprecise_dtypes=True), [], [("LL0", 0, V)])
+    op("g", lambda e: e.iota(T.LO[:], [[1, 256]], 0, 0, allow_small_or_imprecise_dtypes=True), [], [full("LO")])
     op("g", sel(T.ID[:], one, [[-1, 128]], A.is_equal, 0, 1), [full("ONE")], [full("ID")])
+    op("g", sel(T.ZL[:], T.ONE[:], [[-16, 9], [1000, 16]], A.is_equal, -15000, 1), [full("ONE")], [full("ZL")])
+    op("g", sel(T.ZB[:], T.ZL[:], [[-16, 9], [1000, 16]], A.not_equal, -15001, 1, 256.0), [full("ZL")], [full("ZB")])
     op("g", sel(T.B1[:], one, [[-16, 8], [0, 16]], A.is_ge, 0, 1), [full("ONE")], [full("B1")])
     op("g", sel(T.BO[:], T.B1[:], [[16, 8], [0, 16]], A.is_ge, 15, -1), [full("B1")], [full("BO")])
     for z in range(4):
@@ -156,91 +238,105 @@ def rank_program(g, core, T, topo):
     for a in range(4):
         op("g", sel(T.LE[:, a, :], one, [[-16, 8], [0, 4], [-1, 4]], A.is_equal, -4 * a, 1), [full("ONE")], [("LE", 128 * a, 128 * a + 128)])
 
-    ts(T.PC[:, 3:4], T.PC[:, 0:1], 15, None, A.bitwise_and, None, [("PC", 0, 1)], [("PC", 3, 4)])
-    ts(T.PC[:, 2:3], T.PC[:, 0:1], 2, 3, A.logical_shift_right, A.bitwise_and, [("PC", 0, 1)], [("PC", 2, 3)])
-    op("v", lambda e: e.tensor_copy(T.CF[:, 3:4], T.PC[:, 3:4]), [("PC", 3, 4)], [("CF", 3, 4)])
-    op("v", lambda e: e.tensor_copy(T.CF[:, 0:1], T.PC[:, 2:3]), [("PC", 2, 3)], [("CF", 0, 1)])
-    ts(T.CI[:], T.RQ[:], T.CF[:, 3:4], None, A.is_equal, None, [full("RQ"), ("CF", 3, 4)], [full("CI")])
-    for a in range(4):
-        op("v", lambda e: e.memset(T.Q4[:, a::4], float(a)), [], [full("Q4")])
-    op("v", lambda e: e.memset(T.RS[:], 1.0), [], [full("RS")])
-    ts(T.MK[:], T.Q4[:], T.CF[:, 0:1], None, A.is_equal, None, [full("Q4"), ("CF", 0, 1)], [full("MK")])
-    op("v", lambda e: e.memset(T.RS[:, 0::4], 0.0), [], [full("RS")], waw=True)
-    for i in range(16):
-        cp(T.DI[:, i, :], T.IF[:], [full("IF"), full("CI")], [("DI", 128 * i, 128 * i + 128)], scale=T.CI[:, i:i + 1])
-    op("v", lambda e: e.tensor_copy(T.EU16[:], T.EUI[:]), [full("EUI")], [full("EU16")])
-    ts(T.PC[:, 1:2], T.PC[:, 0:1], 3, None, A.bitwise_and, None, [("PC", 0, 1)], [("PC", 1, 2)])
-    op("v", lambda e: e.tensor_copy(T.EV16[:], T.EVI[:]), [full("EVI")], [full("EV16")])
-    op("v", lambda e: e.tensor_tensor(T.CF[:, 1:2], T.PC[:, 2:3], T.PC[:, 1:2], A.is_ge), [("PC", 1, 3)], [("CF", 1, 2)])
-    ts(T.CF[:, 2:3], T.CF[:, 1:2], -0.5, None, A.add, None, [("CF", 1, 2)], [("CF", 2, 3)])
-    op("v", lambda e: e.tensor_copy(T.C4[:, 11:12], T.PC[:, 1:2]), [("PC", 1, 2)], [("C4", 11, 12)])
+    P0 = [("PC", 0, 1)]
+    ts(T.PC[:, 3:4], T.PC[:, 0:1], 1, None, A.bitwise_and, None, P0, [("PC", 3, 4)])
+    ts(T.PC[:, 2:3], T.PC[:, 0:1], 2, 3, A.logical_shift_right, A.bitwise_and, P0, [("PC", 2, 3)])
+    ts(T.PC[:, 1:2], T.PC[:, 0:1], 3, None, A.bitwise_and, None, P0, [("PC", 1, 2)])
+    tc(T.CF[:, 3:4], T.PC[:, 3:4], [("PC", 3, 4)], [("CF", 3, 4)])
+    tc(T.CF[:, 0:1], T.PC[:, 2:3], [("PC", 2, 3)], [("CF", 0, 1)])
+    tc(T.C4[:, 11:12], T.PC[:, 1:2], [("PC", 1, 2)], [("C4", 11, 12)])
+    ts(T.CF[:, 4:5], T.CF[:, 3:4], -1.0, 1.0, A.mult, A.add, [("CF", 3, 4)], [("CF", 4, 5)])
+    ts(T.QH[:], T.RQ[:], T.CF[:, 3:4], None, A.mult, None, [full("RQ"), ("CF", 3, 4)], [full("QH")])
     ts(T.C4[:, 0:4], T.RQ[:, 0:4], T.CF[:, 0:1], None, A.is_equal, None, [full("RQ"), ("CF", 0, 1)], [("C4", 0, 4)])
     ts(T.C4[:, 4:8], T.RQ[:, 0:4], T.C4[:, 11:12], None, A.is_equal, None, [full("RQ"), ("C4", 11, 12)], [("C4", 4, 8)])
-    op("v", lambda e: e.tensor_tensor(T.CK[:], T.C4[:, 0:4], T.C4[:, 4:8], A.subtract), [("C4", 0, 8)], [full("CK")])
-    op("v", lambda e: e.tensor_copy(T.EVF[:], T.EVI[:]), [full("EVI")], [full("EVF")])
-    cp(T.IE[:], T.LL0[:, 0:E], [("LL0", 0, E)], [full("IE")])
-    for k in range(4):
-        cp(T.CD[:, k, :], T.ID[:], [full("ID"), full("CK")], [("CD", 128 * k, 128 * k + 128)], scale=T.CK[:, k:k + 1])
-    mm(T.DB[:], T.BO[:], T.CD[:], True, True, [full("BO"), full("CD")], [full("DB")])
-    cp(T.LD[:], T.DB[:], [full("DB")], [full("LD")])
-    for z in range(4):
-        mm(T.MR3[:, z::4], T.LV[:, z, :], T.EVF[:], True, True, [("LV", 128 * z, 128 * z + 128), full("EVF")], [full("MR3")])
-    cp(T.VW[:], T.MR3[:], [full("MR3")], [full("VW")])
-    for a in range(4):
-        mm(T.CX[:, 128 * a:128 * a + 128], T.LE[:, a, :], T.IF[:], True, True, [("LE", 128 * a, 128 * a + 128), full("IF")], [full("CX")])
+    tt(T.CF[:, 1:2], T.PC[:, 2:3], T.PC[:, 1:2], A.is_ge, [("PC", 1, 3)], [("CF", 1, 2)])
+    tt(T.CK[:], T.C4[:, 0:4], T.C4[:, 4:8], A.subtract, [("C4", 0, 8)], [full("CK")])
+    ts(T.CF[:, 2:3], T.CF[:, 1:2], -0.5, None, A.add, None, [("CF", 1, 2)], [("CF", 2, 3)])
+    hold[0] = here()
 
-    def ring_list(b):
-        if b == 0:
-            win, off, rd = T.RI[:], T.EU16[:, 0:32], [full("RI"), ("EU16", 0, 128)]
+    def digits(q, out, n, reg):
+        rd = [full("LO"), ("CF", 4, 5), ("QH", n, n + 1)]
+        if q == "v":
+            ts(out, T.LO[:], T.CF[:, 4:5], T.QH[:, n:n + 1], A.mult, A.add, rd, [reg], n=128)
         else:
-            n = V + E * b
-            win, off, rd = T.RW[:, 0:n], T["LW%d" % (b - 1)][:, 64:96], [("RW", 0, n), ("LW%d" % (b - 1), 64, 96)]
-        op("v", lambda e: e.tensor_tensor(T.XM[:], win.indirect(off), T.MK[:], A.mult), rd + [full("MK")], [full("XM")])
-        op("v", lambda e: e.tensor_tensor_scan(T.XS[:], T.RS[:], T.XM[:], 0.0, A.mult, A.add), [full("RS"), full("XM")], [full("XS")])
-        op("v", lambda e: e.tensor_copy(T["OF%d" % b][:], T.XS[:, 3::4]), [full("XS")], [full("OF%d" % b)])
+            op("s", lambda e: e.activation(out, T.LO[:], F.Identity, bias=T.QH[:, n:n + 1], scale=T.CF[:, 4:5]), rd, [reg], n=256)
 
-    def ring_diff(b):
-        op("v", lambda e: e.tensor_tensor(T.DF[:], T.VW[:, 128 * b:128 * b + 128], T.XS[:, 3::4], A.subtract),
-           [("VW", 128 * b, 128 * b + 128), full("XS")], [full("DF")])
+    for n in range(4):
+        digits("v", T.LL0[:, 256 * n:256 * n + 256], n, ("LL0", 256 * n, 256 * n + 256))
+    hold[0] = None
+    for n in range(8):
+        digits("vs"[n > 1], T.PZ[:, 256 * n:256 * n + 256], n + 4, ("PZ", 256 * n, 256 * n + 256))
+    cp(T.IF[:], T.ID[:], [full("ID")], [full("IF")])
+    cp(T.NI[:], T.ID[:], [full("ID")], [full("NI")], scale=-1.0)
+    for a in range(4):
+        cp(T.RD[:, a, :], T.ID[:], [full("ID"), ("C4", 0, 4)], [("RD", 128 * a, 128 * a + 128)], scale=T.C4[:, a:a + 1])
+    tc(T.EU16[:], T.EUI[:], [full("EUI")], [full("EU16")], n=128)
 
-    def place_scatter(b):
-        ll = "LL%d" % (b % 2)
-        op("v", lambda e: e.tensor_scalar(T[ll][:, 0:V].indirect(T.EU16[:, 32 * b:32 * b + 32]), T.IE[:], 1.0, float(V + E * b), A.mult, A.add),
-           [full("IE"), ("EU16", 0, 128)], [(ll, 0, V)], waw=True)
+    def place_scatter(b, h0, h1):
+        ll = "LL%d" % b
+        for h in range(h0, h1):
+            src = T.PZ[:, E * b + 256 * h:E * b + 256 * h + 256]
+            dst = T[ll][:, 0:V].indirect(T.EU16[:, 32 * b + 16 * h:32 * b + 16 * h + 16])
+            op("v", lambda e, dst=dst, src=src: e.tensor_copy(dst, src), [("PZ", E * b, E * b + E), ("EU16", 0, 128)], [(ll, 0, V)], waw=True, t=0.80)
+        if h1 == 2 and b + 1 < NB:
+            dmas([("y", T["LL%d" % (b + 1)][:, 0:V], T[ll][:, 0:V])], [(ll, 0, V)], [("LL%d" % (b + 1), 0, V)])
 
     def place_next(b):
-        ll = "LL%d" % (b % 2)
-        if b < NB - 1:
-            gath("s", T[ll][:, V:V + E], T[ll][:, 0:V], T.EU16[:, 32 * b + 32:32 * b + 64], [(ll, 0, V), ("EU16", 0, 128)], [(ll, V, V + E)])
+        ll = "LL%d" % b
+        gath("s", T[ll][:, V:V + E], T[ll][:, 0:V], T.EU16[:, 32 * b + 32:32 * b + 64], [(ll, 0, V), ("EU16", 0, 128)], [(ll, V, V + E)])
 
-    def place_mm(b, i0, i1):
-        if b >= NB:
-            return
-        n, ll = 96 if b < NB - 1 else 64, "LL%d" % (b % 2)
-        for i in range(i0, i1):
-            mm(T.LX[:, 0:n], T.DI[:, i, :], T[ll][:, i:16 * n:16], i == 0, i == 15, [("DI", 128 * i, 128 * i + 128), (ll, 0, 16 * n)], [("LX", 0, n)])
+    def place_mm(b, part):
+        ll, lx, c0, n = "LL%d" % b, ("LX", "LN", "LX")[part], (0, V, 0)[part], (64, 32, 96)[part]
+        for i in range(16):
+            mm(T[lx][:, 0:n], T.ZB[:, 15 - i:143 - i], T[ll][:, c0 + i:c0 + 16 * n:16], i == 0, i == 15, [full("ZB"), (ll, c0, c0 + 16 * n)], [(lx, 0, n)], n=n)
 
-    def place_out(b):
-        n = 96 if b < NB - 1 else 64
-        op("v", lambda e: e.tensor_copy(T["LW%d" % b][:, 0:n], T.LX[:, 0:n]), [("LX", 0, n)], [("LW%d" % b, 0, n)])
+    def place_out(b, part):
+        o, lx, n, c0 = "LW%d" % b, ("LX", "LN", "LX")[part], (64, 32, 96)[part], (0, 64, 0)[part]
+        tc(T[o][:, c0:c0 + n], T[lx][:, 0:n], [(lx, 0, n)], [(o, c0, c0 + n)], n=n)
+
+    def ring_gather(b, h):
+        g0 = 256 * h
+        if b == 0:
+            gath("s", T.GR[:, g0:g0 + 256], T.RW[:, 0:V], T.EU16[:, 16 * h:16 * h + 16], [("RW", 0, V), ("EU16", 0, 128)], [("GR", g0, g0 + 256)])
+        else:
+            n, lu = V + E * b, "LW%d" % (b - 1)
+            gath("s", T.GR[:, g0:g0 + 256], T.RW[:, 0:n], T[lu][:, 64 + 16 * h:80 + 16 * h], [("RW", 0, n), (lu, 64, 96)], [("GR", g0, g0 + 256)])
+
+    def ring_sum(h):
+        cx, g0 = "CX%d" % h, 256 * h
+        for a in range(4):
+            mm(T[cx][:, 0:64], T.RD[:, a, :], T.GR[:, g0 + a:g0 + 256:4], a == 0, a == 3, [("RD", 128 * a, 128 * a + 128), ("GR", g0, g0 + 256)], [(cx, 0, 64)], n=256)
+
+    def ring_out(b, h):
+        of, cx = "OF%d" % b, "CX%d" % h
+        tc(T[of][:, 64 * h:64 * h + 64], T[cx][:, 0:64], [(cx, 0, 64)], [(of, 64 * h, 64 * h + 64)])
+
+    def ring_diff(b, h):
+        c0 = 128 * b + 64 * h
+        tt(T.DF[:, 64 * h:64 * h + 64], T.VW[:, c0:c0 + 64], T["CX%d" % h][:, 0:64], A.subtract, [("VW", c0, c0 + 64), ("CX%d" % h, 0, 64)], [("DF", 64 * h, 64 * h + 64)])
 
     def mem_u(b):
-        mu = "MU%d" % (b % 2)
-        if b == 0:
-            gath("s", T[mu][:], T.TB0[:, own:own + V], T.EU16[:, 0:32], [("TB0", own, own + V), ("EU16", 0, 128)], [full(mu)])
-        else:
-            n = V + E * b
-            gath("s", T[mu][:], T.OB[:, 0:n], T["LW%d" % (b - 1)][:, 64:96], [("OB", 0, n), ("LW%d" % (b - 1), 64, 96)], [full(mu)])
+        tb, mu = "TB%d" % b, "MU%d" % (b % 2)
+        gath("s", T[mu][:], T[tb][:, own:own + V], T.EU16[:, 32 * b:32 * b + 32], [(tb, own, own + V), ("EU16", 0, 128)], [full(mu)])
 
-    def block_half(b, h, q, dst, base):
-        n = V + E * (b + 1)
-        return gath(q, T[dst][:, base + 512 * h:base + 512 * h + 512], T.OB[:, 0:n], T["LW%d" % b][:, 32 * h:32 * h + 32],
-                    [("OB", 0, n), ("LW%d" % b, 0, 64)], [(dst, base + 512 * h, base + 512 * h + 512)])
+    def mem_v(b):
+        tb, mv = "TB%d" % b, "MV%d" % (b % 2)
+        gath("s", T[mv][:], T[tb][:], T.EV16[:, 32 * b:32 * b + 32], [full(tb), ("EV16", 0, 128)], [full(mv)])
+        marks["mv"] = here()
+
+    def wadd(b, name, start):
+        src = name + "%d" % (b % 2)
+        for h in range(2):
+            mm(T["W%d" % h][:, 0:256], T.ID[:], T[src][:, 256 * h:256 * h + 256], start, False, [full("ID"), full(src)], [("W%d" % h, 0, 256)], n=256)
+
+    def block_half(b, h, dst, base):
+        n, c0 = V + E * (b + 1), base + 512 * h
+        op("s", lambda e: e.activation(T[dst][:, c0:c0 + 512], T.OB[:, 0:n].indirect(T["LW%d" % b][:, 32 * h:32 * h + 32]), F.Relu, bias=15.0, scale=-1.0),
+           [("OB", 0, n), ("LW%d" % b, 0, 64)], [(dst, c0, c0 + 512)], t=0.73)
 
     def send_half(b, h):
         tb = "TB%d" % (b + 1)
         c0 = own + 512 * h
-        order("g", [(tb, c0, c0 + 512)], [])
         ap = T[tb][:, c0:c0 + 512]
         mask = topo.mask(core, peers[0])
         ids = []
@@ -249,155 +345,258 @@ def rank_program(g, core, T, topo):
             mask &= topo.mask(core, p)
             ids.append(DstId(rid=rid, pnc=pid))
         ne = bin(mask).count("1")
-        g.remote_dma_fused([RemoteDMATransfer(dst_ids=ids, dma_engine_mask=mask, remote_sem=T.sem["arr%d" % b],
-                                              srcs=[ap], dsts=[ap] * len(ids))], local_sem=T.sem.sent)
-        total["sent"] = total.get("sent", 0) + ne
-        if h == 1:
+
+        def send():
+            g.remote_dma_fused([RemoteDMATransfer(dst_ids=ids, dma_engine_mask=mask, remote_sem=T.sem["arr%d" % b],
+                                                  srcs=[ap], dsts=[ap] * len(ids))], local_sem=T.sem.sent)
+            total["sent"] = total.get("sent", 0) + ne
+
+        def arrive():
             total["arr%d" % b] = 2 * ne * len(peers)
-            rec = ("arr%d" % b, total["arr%d" % b], {})
             for p in peers:
                 o = T.rank_of(p) * V
-                note("far", rec, [], [(tb, o, o + V)])
+                note("far", ("arr%d" % b, total["arr%d" % b], {}), [], [(tb, o, o + V)])
 
-    ring_list(0)
-    place_scatter(0)
-    cp(T.LL1[:, 0:V], T.LL0[:, 0:V], [("LL0", 0, V)], [("LL1", 0, V)])
-    place_next(0)
-    op("v", lambda e: e.tensor_copy(T.RW[:, 0:V], T.RI[:]), [full("RI")], [("RW", 0, V)])
-    place_scatter(1)
+        item(q="g", kind="send", fn=send, reads=[(tb, c0, c0 + 512)], writes=[("sends%d" % b, h, h + 1)], time=0.5, lag=0.0)
+        if h == 1:
+            item(q="far", kind="far", fn=arrive, reads=[("sends%d" % b, 0, 2)], writes=[(tb, T.rank_of(p) * V, T.rank_of(p) * V + V) for p in peers], time=0.0, lag=FAR)
+
+    place_scatter(0, 0, 1)
+    tc(T.EVF[:], T.EVI[:], [full("EVI")], [full("EVF")], n=128)
+    hold[0] = here()
+    place_scatter(0, 1, 2)
+    hold[0] = None
+    for k in range(3):
+        cp(T.CD[:, k, :], T.ID[:], [full("ID"), full("CK")], [("CD", 128 * k, 128 * k + 128)], scale=T.CK[:, k + 1:k + 2])
+    mm(T.DA0[:, 0:384], T.BO[:], T.CD[:], True, True, [full("BO"), full("CD")], [("DA0", 0, 384)], n=384)
+    for z in range(4):
+        mm(T.DA1[:, z::4], T.LV[:, z, :], T.EVF[:], True, True, [("LV", 128 * z, 128 * z + 128), full("EVF")], [full("DA1")], n=512)
+    cp(T.LD[:], T.DA0[:, 0:384], [("DA0", 0, 384)], [full("LD")], n=384)
+    hold[0] = here()
+    cp(T.VW[:], T.DA1[:], [full("DA1")], [full("VW")], n=512)
+    hold[0] = None
+    vw = here()
+    place_mm(0, 0)
+    tc(T.RW[:, 0:V], T.RI[:], [full("RI")], [("RW", 0, V)], n=V)
+    hold[0] = vw
+    ring_gather(0, 0)
+    hold[0] = None
+    ring_gather(0, 1)
+    r0 = here()
+    ring_sum(0)
+    ring_sum(1)
+    tc(T.EV16[:], T.EVI[:], [full("EVI")], [full("EV16")], n=128)
+    op("v", lambda e: e.memset(T.RS[:], 1.0), [], [full("RS")], n=512)
+    op("v", lambda e: e.memset(T.RS[:, 0::4], 0.0), [], [full("RS")], waw=True, n=128)
+    ring_out(0, 0)
+    ring_out(0, 1)
+    hold[0] = r0
     mem_u(0)
-    place_mm(0, 0, PL0[0])
+    hold[0] = here()
+    mem_v(0)
+    hold[0] = None
+    ts(T.OB[:, 0:V], T.TB0[:, own:own + V], -1.0, 15.0, A.mult, A.add, [("TB0", own, own + V)], [("OB", 0, V)], n=V // 2)
+    wadd(0, "MU", True)
+    for a in range(4):
+        mm(T.LN[:, 128 * a:128 * a + 128], T.LE[:, a, :], T.IF[:], True, True, [("LE", 128 * a, 128 * a + 128), full("IF")], [full("LN")], n=512)
+    place_out(0, 0)
 
     for b in range(NB):
         last = b == NB - 1
-        tb, mt, mu, mv = "TB%d" % b, "MT%d" % (b % 2), "MU%d" % (b % 2), "MV%d" % (b % 2)
-        pl = PL1 if b == 0 else PL
+        tb, mt, mv, of = "TB%d" % b, "MT%d" % (b % 2), "MV%d" % (b % 2), "OF%d" % b
 
-        def lmm(j):
-            place_mm(b + 1, pl[j], pl[j + 1])
+        def slots(c, q):
+            s = 512 * c
+            gath(q, T[mt][:, s:s + 512], T[tb][:], T[of][:, 32 * c:32 * c + 32], [full(tb), (of, 32 * c, 32 * c + 32)], [(mt, s, s + 512)])
 
-        def scan(c):
-            s = (512 * c, 512 * c + 512)
-            op("v", lambda e: e.tensor_tensor_scan(T.MX[:, s[0]:s[1]], T.RS[:], T[mt][:, s[0]:s[1]], 0.0, A.mult, A.max),
-               [full("RS"), (mt,) + s], [("MX",) + s])
+        def scan(c0, c1):
+            s = (512 * c0, 512 * c1)
+            n = s[1] - s[0]
+            x = T[mt][:, s[0]:s[1]]
+            op("v", lambda e: e.tensor_tensor_scan(T.MX[:, s[0]:s[1]], T.RS[:, 0:n], x, 0.0, A.mult, A.max),
+               [full("RS"), (mt,) + s], [("MX",) + s], n=n // 2)
 
-        def prod(c):
-            s = (512 * c, 512 * c + 512)
-            op("v", lambda e: e.tensor_tensor(T.PR[:, s[0]:s[1]], T["MR%d" % c][:], T[mt][:, s[0]:s[1]], A.mult), [full("MR%d" % c), (mt,) + s], [("PR",) + s])
-            db, d0 = ("DB", "DB", "MR0", "MR0")[c], (0, 128, 0, 128)[c]
-            for k in range(4):
-                mm(T[db][:, d0:d0 + 128], T.LD[:, k, :], T.PR[:, s[0] + k:s[1]:4], k == 0, k == 3, [full("LD"), ("PR",) + s], [(db, d0, d0 + 128)])
+        def wsub(h):
+            s = (1024 * h, 1024 * h + 1024)
+            mm(T["W%d" % h][:, 0:256], T.NI[:], T.MX[:, s[0] + 3:s[1]:4], False, True, [full("NI"), ("MX",) + s], [("W%d" % h, 0, 256)], n=256)
 
-        def sub(c0, c1):
-            e0, e1 = 128 * c0, 128 * c1
-            op("v", lambda e: e.tensor_tensor(T.SS[:, e0:e1], T.W[:, e0:e1], T.MX[:, 4 * e0 + 3:4 * e1:4], A.subtract), [full("W"), ("MX", 4 * e0, 4 * e1)], [("SS", e0, e1)])
+        def clip(h):
+            o, w = V + E * b + 256 * h, "W%d" % h
+            op("s", lambda e: e.activation(T.OB[:, o:o + 256], T[w][:, 0:256], F.Relu, bias=15.0, scale=-1.0), [(w, 0, 256)], [("OB", o, o + 256)], n=256)
 
-        def clip(c0, c1):
-            e0, e1 = 128 * c0, 128 * c1
-            o = V + E * b
-            ts(T.OB[:, o + e0:o + e1], T.SS[:, e0:e1], 0.0, 15.0, A.max, A.min, [("SS", e0, e1)], [("OB", o + e0, o + e1)])
+        def where(h, j):
+            return (("DA%d" % h, 0), ("DA%d" % h, 256), ("CX%d" % h, 256))[j]
 
-        def lowest(h):
-            db, cx = ("DB", "MR0")[h], ("CX", "MR2")[h]
-            ts(T.SG[:, 256 * h:256 * h + 256], T[db][:, 0:256], T.CF[:, 2:3], 0.0, A.add, A.is_gt, [(db, 0, 256), ("CF", 2, 3)], [("SG", 256 * h, 256 * h + 256)])
+        def diff(h):
+            s = (1024 * h, 1024 * h + 1024)
+            for j in range(3):
+                bk, d = where(h, j)
+                for w, k in (("ID", j + 1), ("NI", 0)):
+                    mm(T[bk][:, d:d + 256], T[w][:], T[mt][:, s[0] + k:s[1]:4], w == "ID", w == "NI", [full(w), (mt,) + s], [(bk, d, d + 256)], n=256)
+
+        def prod(h, j):
+            bk, d = where(h, j)
+            p = 256 * (3 * h + j)
+            tt(T.PR[:, p:p + 256], T[bk][:, d:d + 256], T[mv][:, 256 * h:256 * h + 256], A.mult, [(bk, d, d + 256), full(mv)], [("PR", p, p + 256)], n=256)
+
+        def cdiff(h):
+            bk = "DA%d" % h
+            for j in range(3):
+                p = 256 * (3 * h + j)
+                mm(T[bk][:, 0:256], T.LD[:, j, :], T.PR[:, p:p + 256], j == 0, j == 2, [full("LD"), ("PR", p, p + 256)], [(bk, 0, 256)], n=256)
+
+        def sign(h):
+            bk = "DA%d" % h
+            op("s", lambda e: e.activation(T.SG[:, 256 * h:256 * h + 256], T[bk][:, 0:256], F.Sign, bias=T.CF[:, 2:3]),
+               [(bk, 0, 256), ("CF", 2, 3)], [("SG", 256 * h, 256 * h + 256)], n=256)
+
+        def count(h):
+            cx, s = "CX%d" % h, 256 * h
             for a in range(4):
-                mm(T[cx][:, 0:64], T.LS[:, a, :], T.SG[:, 256 * h + a:256 * h + 256:4], a == 0, a == 3, [full("LS"), ("SG", 256 * h, 256 * h + 256)], [(cx, 0, 64)])
+                mm(T[cx][:, 0:64], T.LS[:, a, :], T.SG[:, s + a:s + 256:4], a == 0, a == 3, [full("LS"), ("SG", s, s + 256)], [(cx, 0, 64)], n=64)
 
         def pick(h):
-            cx = ("CX", "MR2")[h]
-            c0, c1, t = 64 * h, 64 * h + 64, 128 * h
-            ts(T.MR1[:, t:t + 64], T[cx][:, 0:64], 3.5, None, A.is_ge, None, [(cx, 0, 64)], [("MR1", t, t + 64)])
-            op("v", lambda e: e.tensor_tensor(T.MR1[:, t + 64:t + 128], T.MR1[:, t:t + 64], T.DF[:, c0:c1], A.mult), [("MR1", t, t + 64), full("DF")], [("MR1", t + 64, t + 128)])
-            op("v", lambda e: e.tensor_tensor(T.ON[:, c0:c1], T.MR1[:, t + 64:t + 128], T.XS[:, 256 * h + 3:256 * h + 256:4], A.add), [("MR1", t + 64, t + 128), full("XS")], [("ON", c0, c1)])
+            cx, c0 = "CX%d" % h, 64 * h
+            ts(T[cx][:, 64:128], T[cx][:, 0:64], 3.0, None, A.is_ge, None, [(cx, 0, 64)], [(cx, 64, 128)])
+            tt(T.ON[:, c0:c0 + 64], T[cx][:, 64:128], T.DF[:, c0:c0 + 64], A.mult, [(cx, 64, 128), ("DF", c0, c0 + 64)], [("ON", c0, c0 + 64)])
+
+        def spread(h):
+            ex, c0 = "W%d" % h, 64 * h
+            for a in range(4):
+                mm(T[ex][:, a:256:4], T.LE[:, a, :], T.ON[:, c0:c0 + 64], True, True, [("LE", 128 * a, 128 * a + 128), ("ON", c0, c0 + 64)], [(ex, 0, 256)], n=256)
 
         def renew(h):
-            ex, c0, c1 = ("CX", "MR3")[h], 64 * h, 64 * h + 64
-            for a in range(4):
-                mm(T[ex][:, a:256:4], T.LE[:, a, :], T.ON[:, c0:c1], True, True, [("LE", 128 * a, 128 * a + 128), ("ON", c0, c1)], [(ex, 0, 256)])
-            o = V + E * b + 256 * h
-            cp(T.RW[:, o:o + 256], T[ex][:, 0:256], [(ex, 0, 256)], [("RW", o, o + 256)])
+            ex, o, g0 = "W%d" % h, V + E * b + 256 * h, 256 * h
+            tt(T.RW[:, o:o + 256], T[ex][:, 0:256], T.GR[:, g0:g0 + 256], A.add, [(ex, 0, 256), ("GR", g0, g0 + 256)], [("RW", o, o + 256)], n=256)
 
-        mm(T.W[:], T.ID[:], T[mu][:], True, False, [full("ID"), full(mu)], [full("W")])
-        gath("s", T[mv][:], T[tb][:], T.EV16[:, 32 * b:32 * b + 32], [full(tb), ("EV16", 0, 128)], [full(mv)])
-        for c in range(4):
-            gath("v" if c == 0 else "s", T[mt][:, 512 * c:512 * c + 512], T[tb][:], T["OF%d" % b][:, 32 * c:32 * c + 32], [full(tb), full("OF%d" % b)], [(mt, 512 * c, 512 * c + 512)])
-        for c in range(4):
-            for k in range(4):
-                mm(T["MR%d" % c][:, k::4], T.ID[:], T[mv][:, 128 * c:128 * c + 128], True, True, [full("ID"), full(mv)], [full("MR%d" % c)])
-            if c == 1:
-                mm(T.W[:], T.ID[:], T[mv][:], False, True, [full("ID"), full(mv)], [full("W")])
+        if b:
+            hold[0] = marks["ring"]
+            mem_v(b)
+        hold[0] = marks["mv"]
+        slots(0, "v")
+        slots(1, "s")
+        slots(2, "s")
+        s2 = here()
+        slots(3, "v")
+        hold[0] = None
         if b == 0:
-            place_next(1)
-            cp(T.LS[:], T.CX[:], [full("CX")], [full("LS")])
-            place_mm(0, PL0[0], PL0[1])
-        else:
-            place_out(b)
+            hold[0] = s2
+            cp(T.LS[:], T.LN[:], [full("LN")], [full("LS")], n=512)
+            hold[0] = None
+        wadd(b, "MV", False)
         if last:
-            scan(0)
-            prod(0)
-            prod(1)
-            scan(1)
-            prod(2)
-            prod(3)
-            lowest(0)
-            ring_diff(b)
-            scan(2)
-            lowest(1)
+            diff(0)
+            scan(0, 2)
+            ring_diff(b, 0)
+            ring_diff(b, 1)
+            for j in (2, 0, 1):
+                prod(0, j)
+            p0 = here()
+            diff(1)
+            hold[0] = here()
+            cdiff(0)
+            c0 = here()
+            sign(0)
+            hold[0] = p0
+            for j in (2, 0, 1):
+                prod(1, j)
+            hold[0] = None
+            wsub(0)
+            count(0)
+            hold[0] = c0
+            cdiff(1)
+            hold[0] = None
+            sign(1)
+            scan(2, 4)
+            wsub(1)
+            count(1)
             pick(0)
-            renew(0)
+            place_out(b, 0)
             pick(1)
+            clip(0)
+            clip(1)
+            spread(0)
+            hold[0] = here()
+            spread(1)
+            hold[0] = None
+            renew(0)
             renew(1)
-            scan(3)
-            sub(0, 4)
-            clip(0, 4)
             n = V + E * NB
             for h in range(2):
-                gath("vs"[h], T.YR[:, 512 * h:512 * h + 512], T.RW[:, 0:n], T.LW3[:, 32 * h:32 * h + 32], [("RW", 0, n), ("LW3", 0, 64)], [("YR", 512 * h, 512 * h + 512)])
-                dmas([("ys"[h], T.yr[k::4, 512 * h:512 * h + 512], T.YR[k::16, 512 * h:512 * h + 512]) for k in range(4)], [("YR", 512 * h, 512 * h + 512)], [])
+                gath("sv"[h], T.YR[:, 512 * h:512 * h + 512], T.RW[:, 0:n], T.LW3[:, 32 * h:32 * h + 32], [("RW", 0, n), ("LW3", 0, 64)], [("YR", 512 * h, 512 * h + 512)])
+                dmas([("ys"[k % 2], T.yr[k::4, 512 * h:512 * h + 512], T.YR[k::16, 512 * h:512 * h + 512]) for k in range(4)], [("YR", 512 * h, 512 * h + 512)], [])
             for h in range(2):
-                block_half(b, h, "sv"[h], "YB", 0)
+                block_half(b, h, "YB", 0)
                 dmas([("y", T.ym[:, 512 * h:512 * h + 512], T.YB[:, 512 * h:512 * h + 512])], [("YB", 512 * h, 512 * h + 512)], [])
             continue
-        scan(0)
-        for c in range(1, 4):
-            if c < 3:
-                prod(c - 1)
-            if b == 0 and c < 3:
-                place_mm(0, PL0[c], PL0[c + 1])
-            else:
-                lmm(c)
-            if c < 3:
-                scan(c)
-        sub(0, 3)
-        scan(3)
-        clip(0, 3)
-        if b + 2 < NB:
-            dst, src = "LL%d" % (b % 2), "LL%d" % ((b + 1) % 2)
-            dmas([("y", T[dst][:, 0:V], T[src][:, 0:V])], [(src, 0, V)], [(dst, 0, V)])
-        sub(3, 4)
-        clip(3, 4)
-        if b == 0:
-            place_out(0)
+        diff(0)
+        scan(0, 2)
+        wsub(0)
+        ring_diff(b, 0)
+        ring_diff(b, 1)
+        if b:
+            place_out(b, 2)
+        scan(2, 3)
+        clip(0)
+        scan(3, 4)
+        wsub(1)
+        prod(0, 2)
+        clip(1)
+        diff(1)
         for h in range(2):
-            block_half(b, h, "s", "TB%d" % (b + 1), own)
+            block_half(b, h, "TB%d" % (b + 1), own)
+            blk = here()
             send_half(b, h)
+        if b == 0:
+            hold[0] = blk
+            place_next(b)
+            place_mm(b, 1)
+            hold[0] = None
+            place_out(b, 1)
+        prod(0, 0)
+        prod(0, 1)
+        hold[0] = here()
+        cdiff(0)
+        c0 = here()
+        sign(0)
+        for j in range(3):
+            prod(1, j)
+        hold[0] = None
+        p1 = here()
+        count(0)
+        hold[0] = c0
+        cdiff(1)
+        hold[0] = None
         mem_u(b + 1)
-        lowest(0)
-        lmm(4)
-        prod(2)
-        prod(3)
-        ring_diff(b)
-        lmm(5)
-        lowest(1)
+        sign(1)
+        count(1)
+        hold[0] = p1
+        place_scatter(b + 1, 0, 1)
+        hold[0] = None
         pick(0)
-        renew(0)
+        spread(0)
+        hold[0] = here()
         pick(1)
+        spread(1)
+        hold[0] = None
+        renew(0)
         renew(1)
-        lmm(6)
+        hold[0] = here()
+        place_scatter(b + 1, 1, 2)
+        hold[0] = None
+        ring_gather(b + 1, 0)
+        ring_gather(b + 1, 1)
+        marks["ring"] = here()
+        ring_sum(0)
+        ring_sum(1)
+        wadd(b + 1, "MU", True)
         if b + 2 < NB:
-            place_scatter(b + 2)
-            place_next(b + 2)
-        ring_list(b + 1)
+            place_next(b + 1)
+        place_mm(b + 1, 2 if b + 2 < NB else 0)
+        ring_out(b + 1, 0)
+        ring_out(b + 1, 1)
+    for j in plan():
+        emit(prog[j])
     for s in total:
         if waited.get(s, 0) < total[s]:
             g.wait_ge(T.sem[s], total[s])

from concourse.bass import DstId, RemoteDMATransfer
from concourse.mybir import AluOpType as A, ActivationFunctionType as F

NB, V, E, R = 4, 1024, 512, 4
BF, F32, I32, U16 = "bfloat16", "float32", "int32", "uint16"
LAG, FAR, SLACK = 0.12, 3.7, 0.03

SCRATCH = {
    "OB": ("sbuf", [128, V + NB * E], BF),
    "RW": ("sbuf", [128, V + NB * E], F32),
    "RI": ("sbuf", [128, V], I32),
    "EUI": ("sbuf", [128, 128], I32), "EVI": ("sbuf", [128, 128], I32),
    "EU16": ("sbuf", [128, 128], U16), "EV16": ("sbuf", [128, 128], U16), "EVF": ("sbuf", [128, 128], F32),
    "MX": ("sbuf", [128, 2048], BF), "PR": ("sbuf", [128, 1536], BF),
    "SG": ("sbuf", [128, 512], BF), "ON": ("sbuf", [128, 128], F32),
    "GR": ("sbuf", [128, 512], F32), "DF": ("sbuf", [128, 128], F32),
    "VW": ("sbuf", [128, 512], F32),
    "YB": ("sbuf", [128, V], BF), "YR": ("sbuf", [128, V], F32),
    "ONE": ("sbuf", [128, 144], BF), "ID": ("sbuf", [128, 128], BF), "NI": ("sbuf", [128, 128], BF), "IF": ("sbuf", [128, 128], F32),
    "ZL": ("sbuf", [128, 144], BF), "ZB": ("sbuf", [128, 144], BF), "RQ": ("sbuf", [128, 16], F32), "QH": ("sbuf", [128, 16], F32),
    "LO": ("sbuf", [128, 256], BF), "PZ": ("sbuf", [128, NB * E], BF),
    "LE": ("sbuf", [128, 4, 128], F32), "LV": ("sbuf", [128, 4, 128], F32), "RD": ("sbuf", [128, 4, 128], F32),
    "BO": ("sbuf", [128, 128], BF), "B1": ("sbuf", [128, 128], BF),
    "LD": ("sbuf", [128, 3, 128], BF), "LS": ("sbuf", [128, 4, 128], BF), "CD": ("sbuf", [128, 3, 128], BF),
    "C4": ("sbuf", [128, 12], F32), "CK": ("sbuf", [128, 4], F32),
    "RS": ("sbuf", [128, 1024], BF),
    "PC": ("sbuf", [128, 8], I32), "CF": ("sbuf", [128, 8], F32),
    "W0": ("psum", [128, 512], F32), "W1": ("psum", [128, 512], F32), "LX": ("psum", [128, 512], F32), "LN": ("psum", [128, 512], F32),
    "DA0": ("psum", [128, 512], F32), "DA1": ("psum", [128, 512], F32), "CX0": ("psum", [128, 512], F32), "CX1": ("psum", [128, 512], F32),
}
for _c in range(4):
    SCRATCH["TB%d" % _c] = ("sbuf", [128, 4 * V], BF)
    SCRATCH["OF%d" % _c] = ("sbuf", [128, 128], U16)
    SCRATCH["LW%d" % _c] = ("sbuf", [128, 96], U16)
    SCRATCH["LL%d" % _c] = ("sbuf", [128, V + E], BF)
for _c in range(2):
    SCRATCH["MU%d" % _c] = ("sbuf", [128, 512], BF)
    SCRATCH["MV%d" % _c] = ("sbuf", [128, 512], BF)
    SCRATCH["MT%d" % _c] = ("sbuf", [128, 2048], BF)
NDMA = 20
SEMAPHORES = ["cv", "cs", "cp", "cg", "sent"] + ["arr%d" % b for b in range(NB)] + ["d%d" % i for i in range(NDMA)]


def rank_program(g, core, T, topo):
    rank = T.rank_of(core)
    if rank is None:
        return
    peers = [c for c in T.cores if c != core]
    own = rank * V
    QU = {"v": g.vector, "s": g.scalar, "p": g.tensor, "g": g, "y": g.sync}
    known = {q: {} for q in QU}
    hold, marks, prog = [None], {}, []
    total, waited, acc, ndma, clks = {}, {}, {}, [0], {}
    psum = {n for n in SCRATCH if SCRATCH[n][0] == "psum"}

    def wait(q, rec):
        sem, val, clk = rec
        if known[q].get(sem, 0) >= val:
            return
        QU[q].wait_ge(T.sem[sem], val)
        waited[sem] = max(waited.get(sem, 0), val)
        for s, x in clk.items():
            known[q][s] = max(known[q].get(s, 0), x)
        known[q][sem] = max(known[q].get(sem, 0), val)

    def order(q, reads, writes, dma=False, waw=False):
        deps = []
        for mode, regs in ((0, reads), (1, writes)):
            for (b, c0, c1) in regs:
                for (aq, aw, a0, a1, rec) in acc.get(b, []):
                    ps = b in psum
                    hit = a1 > c0 and c1 > a0
                    if not ps and not hit:
                        continue
                    same = aq == q and not dma
                    if mode == 0 and ((aw and hit) or (ps and not same)):
                        deps.append(rec)
                    elif mode == 1 and (not same or (aw and waw)):
                        deps.append(rec)
        for rec in sorted(deps, key=lambda x: -sum(x[2].values()) - x[1]):
            wait(q, rec)

    def note(q, rec, reads, writes):
        for w, regs in ((False, reads), (True, writes)):
            for (b, c0, c1) in regs:
                lst = acc.setdefault(b, [])
                if w and b not in psum:
                    lst[:] = [x for x in lst if not (c0 <= x[2] and x[3] <= c1)]
                lst.append((q, w, c0, c1, rec))

    def emit(k):
        q, reads, writes = k["q"], k["reads"], k["writes"]
        if k["kind"] == "op":
            order(q, reads, writes, waw=k["waw"])
            sem = "c" + q
            k["fn"](QU[q]).then_inc(T.sem[sem], 1)
            total[sem] = total.get(sem, 0) + 1
            note(q, (sem, total[sem], dict(known[q])), reads, writes)
        elif k["kind"] == "dma":
            order(q, reads, writes, dma=True)
            QU[q].dma_start(*k["fn"]).then_inc(T.sem[k["sem"]], 16)
            total[k["sem"]] = 16 * k["n"]
            clk = clks.setdefault(k["sem"], [0, {}])
            for s, x in known[q].items():
                clk[1][s] = max(clk[1].get(s, 0), x)
            clk[0] += 1
            if clk[0] == k["n"]:
                note("dma" + k["sem"], (k["sem"], total[k["sem"]], clk[1]), reads, writes)
        else:
            if k["kind"] == "send":
                order("g", reads, [])
            k["fn"]()

    def item(**k):
        k["hold"] = hold[0]
        prog.append(k)

    def here():
        return len(prog) - 1

    def op(q, fn, reads, writes, waw=False, n=128, t=None):
        item(q=q, kind="op", fn=fn, reads=reads, writes=writes, waw=waw, time=t or (0.38 if q == "g" else 0.055 + 0.00083 * max(n, 64)), lag=LAG)

    def dmas(parts, reads, writes, lag=2.2):
        sem = "d%d" % ndma[0]
        ndma[0] += 1
        for q, out, in_ in parts:
            item(q=q, kind="dma", fn=(out, in_), reads=reads, writes=writes, time=0.06, lag=lag, sem=sem, n=len(parts))

    def plan():
        n = len(prog)
        after, then = [set() for _ in range(n)], [[] for _ in range(n)]
        seen, bank = {}, {}
        for j, k in enumerate(prog):
            regs = [(0,) + r for r in k["reads"]] + [(1,) + r for r in k["writes"]]
            if k["hold"] is not None and prog[k["hold"]]["q"] == k["q"]:
                after[j].add(k["hold"])
            for w, b, c0, c1 in regs:
                if b in psum:
                    if bank.get(b, j) != j:
                        after[j].add(bank[b])
                    continue
                for (i, w2, a0, a1) in seen.get(b, []):
                    together = k["kind"] == prog[i]["kind"] == "dma" and k["sem"] == prog[i]["sem"]
                    if i != j and (w or w2) and a1 > c0 and c1 > a0 and not together:
                        after[j].add(i)
            for w, b, c0, c1 in regs:
                if b in psum:
                    bank[b] = j
                else:
                    seen.setdefault(b, []).append((j, w, c0, c1))
        for j in range(n):
            for i in after[j]:
                then[i].append(j)
        near = lambda i, j: prog[i]["q"] == prog[j]["q"] == "p"
        way = [0.0] * n
        for j in range(n - 1, -1, -1):
            k = prog[j]
            for i in then[j]:
                way[j] = max(way[j], way[i] - (k["lag"] if near(i, j) else 0))
            way[j] += k["time"] + k["lag"]
        for j in range(n):
            way[j] += 1000.0 - j if prog[j]["kind"] == "dma" else 0.0
        left = [len(after[j]) for j in range(n)]
        ready = {j for j in range(n) if not left[j]}
        at, start, free = [0.0] * n, {}, {}
        while ready:
            best = None
            for j in ready:
                t = max(at[j], free.get(prog[j]["q"], 0.0))
                c = (t - SLACK * way[j], -way[j], j, t)
                if best is None or c < best:
                    best = c
            j, t = best[2], best[3]
            k = prog[j]
            start[j] = t
            free[k["q"]] = t + k["time"]
            ready.discard(j)
            for i in then[j]:
                at[i] = max(at[i], t + k["time"] + (0 if near(i, j) else k["lag"]))
                left[i] -= 1
                if not left[i]:
                    ready.add(i)
        return sorted(range(n), key=lambda j: (start[j], j))

    def full(n):
        c = 1
        for d in SCRATCH[n][1][1:]:
            c *= d
        return (n, 0, c)

    def mm(out, lhsT, rhs, start, stop, reads, writes, n=128):
        op("p", lambda e: e.matmul(out, lhsT, rhs, start, stop), reads, writes, t=0.04 + 0.000417 * max(n, 64))

    def cp(out, in_, reads, writes, scale=1.0, n=128):
        op("s", lambda e: e.activation(out, in_, F.Copy, scale=scale), reads, writes, n=n)

    def gath(q, out, win, off, reads, writes):
        t = 0.06 + 0.0014 * (writes[0][2] - writes[0][1])
        if q == "v":
            return op(q, lambda e: e.tensor_copy(out, win.indirect(off)), reads, writes, t=t)
        return op(q, lambda e: e.activation(out, win.indirect(off), F.Copy), reads, writes, t=t)

    def sel(out, in_, pat, cmp, base, cm, fill=0.0):
        return lambda e: e.affine_select(out, in_, pat, cmp, fill, base, cm)

    def ts(out, in_, s1, s2, o0, o1, reads, writes, n=64):
        if o1 is None:
            op("v", lambda e: e.tensor_scalar(out, in_, s1, None, o0), reads, writes, n=n)
        else:
            op("v", lambda e: e.tensor_scalar(out, in_, s1, s2, o0, o1), reads, writes, n=n)

    def tt(out, x, y, o, reads, writes, n=64):
        op("v", lambda e: e.tensor_tensor(out, x, y, o), reads, writes, n=n)

    def tc(out, in_, reads, writes, n=64):
        op("v", lambda e: e.tensor_copy(out, in_), reads, writes, n=n)

    dmas([("y", T.EUI[:], T.eu[:])], [], [full("EUI")], 2.0)
    dmas([("s", T.EVI[:], T.ev[:])], [], [full("EVI")], 2.0)
    dmas([("sy"[i % 2], T.RI[i::16, :], T.ring0[i % 4::4, :]) for i in range(16)], [], [full("RI")], 3.7)
    dmas([("y", T.TB0[:, own:own + V], T.m0[:, own:own + V])], [], [("TB0", own, own + V)], 4.8)
    rest = [T.rank_of(p) * V for p in peers]
    dmas([("s", T.TB0[:, o:o + V], T.m0[:, o:o + V]) for o in rest], [], [("TB0", o, o + V) for o in rest], 6.6)

    one = T.ONE[:, 0:128]
    op("v", lambda e: e.memset(T.ONE[:], 1.0), [], [full("ONE")])
    op("g", lambda e: e.iota(T.PC[:, 0:1], [[0, 1]], 0, 1), [], [("PC", 0, 1)])
    op("g", lambda e: e.iota(T.RQ[:], [[1, 16]], 0, 0, allow_small_or_imprecise_dtypes=True), [], [full("RQ")])
    op("g", lambda e: e.iota(T.LO[:], [[1, 256]], 0, 0, allow_small_or_imprecise_dtypes=True), [], [full("LO")])
    op("g", sel(T.ID[:], one, [[-1, 128]], A.is_equal, 0, 1), [full("ONE")], [full("ID")])
    op("g", sel(T.ZL[:], T.ONE[:], [[-16, 9], [1000, 16]], A.is_equal, -15000, 1), [full("ONE")], [full("ZL")])
    op("g", sel(T.ZB[:], T.ZL[:], [[-16, 9], [1000, 16]], A.not_equal, -15001, 1, 256.0), [full("ZL")], [full("ZB")])
    op("g", sel(T.B1[:], one, [[-16, 8], [0, 16]], A.is_ge, 0, 1), [full("ONE")], [full("B1")])
    op("g", sel(T.BO[:], T.B1[:], [[16, 8], [0, 16]], A.is_ge, 15, -1), [full("B1")], [full("BO")])
    for z in range(4):
        op("g", sel(T.LV[:, z, :], one, [[-16, 8], [-1, 4], [0, 4]], A.is_equal, -4 * z, 1), [full("ONE")], [("LV", 128 * z, 128 * z + 128)])
    for a in range(4):
        op("g", sel(T.LE[:, a, :], one, [[-16, 8], [0, 4], [-1, 4]], A.is_equal, -4 * a, 1), [full("ONE")], [("LE", 128 * a, 128 * a + 128)])

    P0 = [("PC", 0, 1)]
    ts(T.PC[:, 3:4], T.PC[:, 0:1], 1, None, A.bitwise_and, None, P0, [("PC", 3, 4)])
    ts(T.PC[:, 2:3], T.PC[:, 0:1], 2, 3, A.logical_shift_right, A.bitwise_and, P0, [("PC", 2, 3)])
    ts(T.PC[:, 1:2], T.PC[:, 0:1], 3, None, A.bitwise_and, None, P0, [("PC", 1, 2)])
    tc(T.CF[:, 3:4], T.PC[:, 3:4], [("PC", 3, 4)], [("CF", 3, 4)])
    tc(T.CF[:, 0:1], T.PC[:, 2:3], [("PC", 2, 3)], [("CF", 0, 1)])
    tc(T.C4[:, 11:12], T.PC[:, 1:2], [("PC", 1, 2)], [("C4", 11, 12)])
    ts(T.CF[:, 4:5], T.CF[:, 3:4], -1.0, 1.0, A.mult, A.add, [("CF", 3, 4)], [("CF", 4, 5)])
    ts(T.QH[:], T.RQ[:], T.CF[:, 3:4], None, A.mult, None, [full("RQ"), ("CF", 3, 4)], [full("QH")])
    ts(T.C4[:, 0:4], T.RQ[:, 0:4], T.CF[:, 0:1], None, A.is_equal, None, [full("RQ"), ("CF", 0, 1)], [("C4", 0, 4)])
    ts(T.C4[:, 4:8], T.RQ[:, 0:4], T.C4[:, 11:12], None, A.is_equal, None, [full("RQ"), ("C4", 11, 12)], [("C4", 4, 8)])
    tt(T.CF[:, 1:2], T.PC[:, 2:3], T.PC[:, 1:2], A.is_ge, [("PC", 1, 3)], [("CF", 1, 2)])
    tt(T.CK[:], T.C4[:, 0:4], T.C4[:, 4:8], A.subtract, [("C4", 0, 8)], [full("CK")])
    ts(T.CF[:, 2:3], T.CF[:, 1:2], -0.5, None, A.add, None, [("CF", 1, 2)], [("CF", 2, 3)])
    hold[0] = here()

    def digits(q, out, n, reg):
        rd = [full("LO"), ("CF", 4, 5), ("QH", n, n + 1)]
        if q == "v":
            ts(out, T.LO[:], T.CF[:, 4:5], T.QH[:, n:n + 1], A.mult, A.add, rd, [reg], n=128)
        else:
            op("s", lambda e: e.activation(out, T.LO[:], F.Identity, bias=T.QH[:, n:n + 1], scale=T.CF[:, 4:5]), rd, [reg], n=256)

    for n in range(4):
        digits("v", T.LL0[:, 256 * n:256 * n + 256], n, ("LL0", 256 * n, 256 * n + 256))
    hold[0] = None
    for n in range(8):
        digits("vs"[n > 1], T.PZ[:, 256 * n:256 * n + 256], n + 4, ("PZ", 256 * n, 256 * n + 256))
    cp(T.IF[:], T.ID[:], [full("ID")], [full("IF")])
    cp(T.NI[:], T.ID[:], [full("ID")], [full("NI")], scale=-1.0)
    for a in range(4):
        cp(T.RD[:, a, :], T.ID[:], [full("ID"), ("C4", 0, 4)], [("RD", 128 * a, 128 * a + 128)], scale=T.C4[:, a:a + 1])
    tc(T.EU16[:], T.EUI[:], [full("EUI")], [full("EU16")], n=128)

    def place_scatter(b, h0, h1):
        ll = "LL%d" % b
        for h in range(h0, h1):
            src = T.PZ[:, E * b + 256 * h:E * b + 256 * h + 256]
            dst = T[ll][:, 0:V].indirect(T.EU16[:, 32 * b + 16 * h:32 * b + 16 * h + 16])
            op("v", lambda e, dst=dst, src=src: e.tensor_copy(dst, src), [("PZ", E * b, E * b + E), ("EU16", 0, 128)], [(ll, 0, V)], waw=True, t=0.80)
        if h1 == 2 and b + 1 < NB:
            dmas([("y", T["LL%d" % (b + 1)][:, 0:V], T[ll][:, 0:V])], [(ll, 0, V)], [("LL%d" % (b + 1), 0, V)])

    def place_next(b):
        ll = "LL%d" % b
        gath("s", T[ll][:, V:V + E], T[ll][:, 0:V], T.EU16[:, 32 * b + 32:32 * b + 64], [(ll, 0, V), ("EU16", 0, 128)], [(ll, V, V + E)])

    def place_mm(b, part):
        ll, lx, c0, n = "LL%d" % b, ("LX", "LN", "LX")[part], (0, V, 0)[part], (64, 32, 96)[part]
        for i in range(16):
            mm(T[lx][:, 0:n], T.ZB[:, 15 - i:143 - i], T[ll][:, c0 + i:c0 + 16 * n:16], i == 0, i == 15, [full("ZB"), (ll, c0, c0 + 16 * n)], [(lx, 0, n)], n=n)

    def place_out(b, part):
        o, lx, n, c0 = "LW%d" % b, ("LX", "LN", "LX")[part], (64, 32, 96)[part], (0, 64, 0)[part]
        tc(T[o][:, c0:c0 + n], T[lx][:, 0:n], [(lx, 0, n)], [(o, c0, c0 + n)], n=n)

    def ring_gather(b, h):
        g0 = 256 * h
        if b == 0:
            gath("s", T.GR[:, g0:g0 + 256], T.RW[:, 0:V], T.EU16[:, 16 * h:16 * h + 16], [("RW", 0, V), ("EU16", 0, 128)], [("GR", g0, g0 + 256)])
        else:
            n, lu = V + E * b, "LW%d" % (b - 1)
            gath("s", T.GR[:, g0:g0 + 256], T.RW[:, 0:n], T[lu][:, 64 + 16 * h:80 + 16 * h], [("RW", 0, n), (lu, 64, 96)], [("GR", g0, g0 + 256)])

    def ring_sum(h):
        cx, g0 = "CX%d" % h, 256 * h
        for a in range(4):
            mm(T[cx][:, 0:64], T.RD[:, a, :], T.GR[:, g0 + a:g0 + 256:4], a == 0, a == 3, [("RD", 128 * a, 128 * a + 128), ("GR", g0, g0 + 256)], [(cx, 0, 64)], n=256)

    def ring_out(b, h):
        of, cx = "OF%d" % b, "CX%d" % h
        tc(T[of][:, 64 * h:64 * h + 64], T[cx][:, 0:64], [(cx, 0, 64)], [(of, 64 * h, 64 * h + 64)])

    def ring_diff(b, h):
        c0 = 128 * b + 64 * h
        tt(T.DF[:, 64 * h:64 * h + 64], T.VW[:, c0:c0 + 64], T["CX%d" % h][:, 0:64], A.subtract, [("VW", c0, c0 + 64), ("CX%d" % h, 0, 64)], [("DF", 64 * h, 64 * h + 64)])

    def mem_u(b):
        tb, mu = "TB%d" % b, "MU%d" % (b % 2)
        gath("s", T[mu][:], T[tb][:, own:own + V], T.EU16[:, 32 * b:32 * b + 32], [(tb, own, own + V), ("EU16", 0, 128)], [full(mu)])

    def mem_v(b):
        tb, mv = "TB%d" % b, "MV%d" % (b % 2)
        gath("s", T[mv][:], T[tb][:], T.EV16[:, 32 * b:32 * b + 32], [full(tb), ("EV16", 0, 128)], [full(mv)])
        marks["mv"] = here()

    def wadd(b, name, start):
        src = name + "%d" % (b % 2)
        for h in range(2):
            mm(T["W%d" % h][:, 0:256], T.ID[:], T[src][:, 256 * h:256 * h + 256], start, False, [full("ID"), full(src)], [("W%d" % h, 0, 256)], n=256)

    def block_half(b, h, dst, base):
        n, c0 = V + E * (b + 1), base + 512 * h
        op("s", lambda e: e.activation(T[dst][:, c0:c0 + 512], T.OB[:, 0:n].indirect(T["LW%d" % b][:, 32 * h:32 * h + 32]), F.Relu, bias=15.0, scale=-1.0),
           [("OB", 0, n), ("LW%d" % b, 0, 64)], [(dst, c0, c0 + 512)], t=0.73)

    def send_half(b, h):
        tb = "TB%d" % (b + 1)
        c0 = own + 512 * h
        ap = T[tb][:, c0:c0 + 512]
        mask = topo.mask(core, peers[0])
        ids = []
        for p in peers:
            rid, pid, _ = topo.addr(p)
            mask &= topo.mask(core, p)
            ids.append(DstId(rid=rid, pnc=pid))
        ne = bin(mask).count("1")

        def send():
            g.remote_dma_fused([RemoteDMATransfer(dst_ids=ids, dma_engine_mask=mask, remote_sem=T.sem["arr%d" % b],
                                                  srcs=[ap], dsts=[ap] * len(ids))], local_sem=T.sem.sent)
            total["sent"] = total.get("sent", 0) + ne

        def arrive():
            total["arr%d" % b] = 2 * ne * len(peers)
            for p in peers:
                o = T.rank_of(p) * V
                note("far", ("arr%d" % b, total["arr%d" % b], {}), [], [(tb, o, o + V)])

        item(q="g", kind="send", fn=send, reads=[(tb, c0, c0 + 512)], writes=[("sends%d" % b, h, h + 1)], time=0.5, lag=0.0)
        if h == 1:
            item(q="far", kind="far", fn=arrive, reads=[("sends%d" % b, 0, 2)], writes=[(tb, T.rank_of(p) * V, T.rank_of(p) * V + V) for p in peers], time=0.0, lag=FAR)

    place_scatter(0, 0, 1)
    tc(T.EVF[:], T.EVI[:], [full("EVI")], [full("EVF")], n=128)
    hold[0] = here()
    place_scatter(0, 1, 2)
    hold[0] = None
    for k in range(3):
        cp(T.CD[:, k, :], T.ID[:], [full("ID"), full("CK")], [("CD", 128 * k, 128 * k + 128)], scale=T.CK[:, k + 1:k + 2])
    mm(T.DA0[:, 0:384], T.BO[:], T.CD[:], True, True, [full("BO"), full("CD")], [("DA0", 0, 384)], n=384)
    for z in range(4):
        mm(T.DA1[:, z::4], T.LV[:, z, :], T.EVF[:], True, True, [("LV", 128 * z, 128 * z + 128), full("EVF")], [full("DA1")], n=512)
    cp(T.LD[:], T.DA0[:, 0:384], [("DA0", 0, 384)], [full("LD")], n=384)
    hold[0] = here()
    cp(T.VW[:], T.DA1[:], [full("DA1")], [full("VW")], n=512)
    hold[0] = None
    vw = here()
    place_mm(0, 0)
    tc(T.RW[:, 0:V], T.RI[:], [full("RI")], [("RW", 0, V)], n=V)
    hold[0] = vw
    ring_gather(0, 0)
    hold[0] = None
    ring_gather(0, 1)
    r0 = here()
    ring_sum(0)
    ring_sum(1)
    tc(T.EV16[:], T.EVI[:], [full("EVI")], [full("EV16")], n=128)
    op("v", lambda e: e.memset(T.RS[:], 1.0), [], [full("RS")], n=512)
    op("v", lambda e: e.memset(T.RS[:, 0::4], 0.0), [], [full("RS")], waw=True, n=128)
    ring_out(0, 0)
    ring_out(0, 1)
    hold[0] = r0
    mem_u(0)
    hold[0] = here()
    mem_v(0)
    hold[0] = None
    ts(T.OB[:, 0:V], T.TB0[:, own:own + V], -1.0, 15.0, A.mult, A.add, [("TB0", own, own + V)], [("OB", 0, V)], n=V // 2)
    wadd(0, "MU", True)
    for a in range(4):
        mm(T.LN[:, 128 * a:128 * a + 128], T.LE[:, a, :], T.IF[:], True, True, [("LE", 128 * a, 128 * a + 128), full("IF")], [full("LN")], n=512)
    place_out(0, 0)

    for b in range(NB):
        last = b == NB - 1
        tb, mt, mv, of = "TB%d" % b, "MT%d" % (b % 2), "MV%d" % (b % 2), "OF%d" % b

        def slots(c, q):
            s = 512 * c
            gath(q, T[mt][:, s:s + 512], T[tb][:], T[of][:, 32 * c:32 * c + 32], [full(tb), (of, 32 * c, 32 * c + 32)], [(mt, s, s + 512)])

        def scan(c0, c1):
            s = (512 * c0, 512 * c1)
            n = s[1] - s[0]
            x = T[mt][:, s[0]:s[1]]
            op("v", lambda e: e.tensor_tensor_scan(T.MX[:, s[0]:s[1]], T.RS[:, 0:n], x, 0.0, A.mult, A.max),
               [full("RS"), (mt,) + s], [("MX",) + s], n=n // 2)

        def wsub(h):
            s = (1024 * h, 1024 * h + 1024)
            mm(T["W%d" % h][:, 0:256], T.NI[:], T.MX[:, s[0] + 3:s[1]:4], False, True, [full("NI"), ("MX",) + s], [("W%d" % h, 0, 256)], n=256)

        def clip(h):
            o, w = V + E * b + 256 * h, "W%d" % h
            op("s", lambda e: e.activation(T.OB[:, o:o + 256], T[w][:, 0:256], F.Relu, bias=15.0, scale=-1.0), [(w, 0, 256)], [("OB", o, o + 256)], n=256)

        def where(h, j):
            return (("DA%d" % h, 0), ("DA%d" % h, 256), ("CX%d" % h, 256))[j]

        def diff(h):
            s = (1024 * h, 1024 * h + 1024)
            for j in range(3):
                bk, d = where(h, j)
                for w, k in (("ID", j + 1), ("NI", 0)):
                    mm(T[bk][:, d:d + 256], T[w][:], T[mt][:, s[0] + k:s[1]:4], w == "ID", w == "NI", [full(w), (mt,) + s], [(bk, d, d + 256)], n=256)

        def prod(h, j):
            bk, d = where(h, j)
            p = 256 * (3 * h + j)
            tt(T.PR[:, p:p + 256], T[bk][:, d:d + 256], T[mv][:, 256 * h:256 * h + 256], A.mult, [(bk, d, d + 256), full(mv)], [("PR", p, p + 256)], n=256)

        def cdiff(h):
            bk = "DA%d" % h
            for j in range(3):
                p = 256 * (3 * h + j)
                mm(T[bk][:, 0:256], T.LD[:, j, :], T.PR[:, p:p + 256], j == 0, j == 2, [full("LD"), ("PR", p, p + 256)], [(bk, 0, 256)], n=256)

        def sign(h):
            bk = "DA%d" % h
            op("s", lambda e: e.activation(T.SG[:, 256 * h:256 * h + 256], T[bk][:, 0:256], F.Sign, bias=T.CF[:, 2:3]),
               [(bk, 0, 256), ("CF", 2, 3)], [("SG", 256 * h, 256 * h + 256)], n=256)

        def count(h):
            cx, s = "CX%d" % h, 256 * h
            for a in range(4):
                mm(T[cx][:, 0:64], T.LS[:, a, :], T.SG[:, s + a:s + 256:4], a == 0, a == 3, [full("LS"), ("SG", s, s + 256)], [(cx, 0, 64)], n=64)

        def pick(h):
            cx, c0 = "CX%d" % h, 64 * h
            ts(T[cx][:, 64:128], T[cx][:, 0:64], 3.0, None, A.is_ge, None, [(cx, 0, 64)], [(cx, 64, 128)])
            tt(T.ON[:, c0:c0 + 64], T[cx][:, 64:128], T.DF[:, c0:c0 + 64], A.mult, [(cx, 64, 128), ("DF", c0, c0 + 64)], [("ON", c0, c0 + 64)])

        def spread(h):
            ex, c0 = "W%d" % h, 64 * h
            for a in range(4):
                mm(T[ex][:, a:256:4], T.LE[:, a, :], T.ON[:, c0:c0 + 64], True, True, [("LE", 128 * a, 128 * a + 128), ("ON", c0, c0 + 64)], [(ex, 0, 256)], n=256)

        def renew(h):
            ex, o, g0 = "W%d" % h, V + E * b + 256 * h, 256 * h
            tt(T.RW[:, o:o + 256], T[ex][:, 0:256], T.GR[:, g0:g0 + 256], A.add, [(ex, 0, 256), ("GR", g0, g0 + 256)], [("RW", o, o + 256)], n=256)

        if b:
            hold[0] = marks["ring"]
            mem_v(b)
        hold[0] = marks["mv"]
        slots(0, "v")
        slots(1, "s")
        slots(2, "s")
        s2 = here()
        slots(3, "v")
        hold[0] = None
        if b == 0:
            hold[0] = s2
            cp(T.LS[:], T.LN[:], [full("LN")], [full("LS")], n=512)
            hold[0] = None
        wadd(b, "MV", False)
        if last:
            diff(0)
            scan(0, 2)
            ring_diff(b, 0)
            ring_diff(b, 1)
            for j in (2, 0, 1):
                prod(0, j)
            p0 = here()
            diff(1)
            hold[0] = here()
            cdiff(0)
            c0 = here()
            sign(0)
            hold[0] = p0
            for j in (2, 0, 1):
                prod(1, j)
            hold[0] = None
            wsub(0)
            count(0)
            hold[0] = c0
            cdiff(1)
            hold[0] = None
            sign(1)
            scan(2, 4)
            wsub(1)
            count(1)
            pick(0)
            place_out(b, 0)
            pick(1)
            clip(0)
            clip(1)
            spread(0)
            hold[0] = here()
            spread(1)
            hold[0] = None
            renew(0)
            renew(1)
            n = V + E * NB
            for h in range(2):
                gath("sv"[h], T.YR[:, 512 * h:512 * h + 512], T.RW[:, 0:n], T.LW3[:, 32 * h:32 * h + 32], [("RW", 0, n), ("LW3", 0, 64)], [("YR", 512 * h, 512 * h + 512)])
                dmas([("ys"[k % 2], T.yr[k::4, 512 * h:512 * h + 512], T.YR[k::16, 512 * h:512 * h + 512]) for k in range(4)], [("YR", 512 * h, 512 * h + 512)], [])
            for h in range(2):
                block_half(b, h, "YB", 0)
                dmas([("y", T.ym[:, 512 * h:512 * h + 512], T.YB[:, 512 * h:512 * h + 512])], [("YB", 512 * h, 512 * h + 512)], [])
            continue
        diff(0)
        scan(0, 2)
        wsub(0)
        ring_diff(b, 0)
        ring_diff(b, 1)
        if b:
            place_out(b, 2)
        scan(2, 3)
        clip(0)
        scan(3, 4)
        wsub(1)
        prod(0, 2)
        clip(1)
        diff(1)
        for h in range(2):
            block_half(b, h, "TB%d" % (b + 1), own)
            blk = here()
            send_half(b, h)
        if b == 0:
            hold[0] = blk
            place_next(b)
            place_mm(b, 1)
            hold[0] = None
            place_out(b, 1)
        prod(0, 0)
        prod(0, 1)
        hold[0] = here()
        cdiff(0)
        c0 = here()
        sign(0)
        for j in range(3):
            prod(1, j)
        hold[0] = None
        p1 = here()
        count(0)
        hold[0] = c0
        cdiff(1)
        hold[0] = None
        mem_u(b + 1)
        sign(1)
        count(1)
        hold[0] = p1
        place_scatter(b + 1, 0, 1)
        hold[0] = None
        pick(0)
        spread(0)
        hold[0] = here()
        pick(1)
        spread(1)
        hold[0] = None
        renew(0)
        renew(1)
        hold[0] = here()
        place_scatter(b + 1, 1, 2)
        hold[0] = None
        ring_gather(b + 1, 0)
        ring_gather(b + 1, 1)
        marks["ring"] = here()
        ring_sum(0)
        ring_sum(1)
        wadd(b + 1, "MU", True)
        if b + 2 < NB:
            place_next(b + 1)
        place_mm(b + 1, 2 if b + 2 < NB else 0)
        ring_out(b + 1, 0)
        ring_out(b + 1, 1)
    for j in plan():
        emit(prog[j])
    for s in total:
        if waited.get(s, 0) < total[s]:
            g.wait_ge(T.sem[s], total[s])
